import numpy as np
import ml_dtypes


def mxq(x, axis, fmt="e4m3"):
    dtype, down = {"e4m3": (ml_dtypes.float8_e4m3fn, 7), "e5m2": (ml_dtypes.float8_e5m2, 14)}[fmt]
    v = np.moveaxis(np.asarray(x, np.float32).astype(ml_dtypes.bfloat16).astype(np.float64), axis, -1)
    blocks = v.reshape(v.shape[:-1] + (-1, 32))
    amax = np.abs(blocks).max(-1, keepdims=True)
    byte = np.maximum(np.where(amax > 0, np.frexp(amax)[1] - 1 + 127, 0) - down, 1)
    scale = np.exp2(byte - 127.0)
    codes = (blocks / scale).astype(np.float32).astype(dtype).astype(np.float64)
    return np.moveaxis((codes * scale).reshape(v.shape), -1, axis)


WIDE = False


def mx_kscale(k):
    if not WIDE:
        return np.ones(k)
    levels = np.array([10, -10, 5, -5, 0])
    if k % 512:
        return np.exp2(np.random.permutation(np.resize(levels, k // 32))).repeat(32)
    a = np.empty((k // 512, 16))
    for p in range(k // 512):
        a[p, :8] = np.random.permutation(np.resize(levels, 8))
        for g in range(8):
            far = levels[np.abs(levels - a[p, g]) >= 10]
            a[p, g + 8] = far[np.random.randint(len(far))]
    return np.exp2(a.ravel()).repeat(32)


def f64(x):
    return np.asarray(x).astype(np.float64)


def striped(idx):
    return np.tile(np.asarray(idx).reshape(-1, 16).T, (8, 1)).astype(np.uint16)


def unstriped(offs):
    return offs[:16].T.reshape(-1).astype(np.int64)


E2M1 = np.array([0.0, 0.5, 1.0, 1.5, 2.0, 3.0, 4.0, 6.0, -0.0, -0.5, -1.0, -1.5, -2.0, -3.0, -4.0, -6.0])


def pack_weight(w, fmt):
    k, n = w.shape
    w = f64(np.asarray(w, np.float32).astype(ml_dtypes.bfloat16)).reshape(k // 32, 32, n)
    amax = np.abs(w).max(1)
    if fmt == "e4m3":
        byte = np.frexp(amax)[1] - 1 + 127 - 7
    else:
        mant, ex = np.frexp(amax / 6.0)
        byte = np.where(mant > 0.5, ex, ex - 1) + 127
    byte = np.clip(np.where(amax > 0, byte, 1), 1, 254)
    scaled = (w * np.exp2(127.0 - byte)[:, None, :]).reshape(k, n).astype(np.float32)
    by_word = np.ascontiguousarray(scaled.reshape(k // 512, 128, 4, n).transpose(0, 1, 3, 2))
    if fmt == "e4m3":
        words = by_word.astype(ml_dtypes.float8_e4m3fn).view(np.uint8)
    else:
        c = by_word.astype(ml_dtypes.float4_e2m1fn).view(np.uint8) & 0xF
        words = (c[..., 0::2] | (c[..., 1::2] << 4)).reshape(k // 512, 128, 2 * n)
    return np.ascontiguousarray(words), np.ascontiguousarray(byte.astype(np.uint8).reshape(k // 512, 16, n))


def unpack_weight(words, scales, fmt):
    g, _, n = scales.shape
    words = np.ascontiguousarray(words).reshape(g, 128, n, -1)
    if fmt == "e4m3":
        vals = words.view(ml_dtypes.float8_e4m3fn).astype(np.float64)
    else:
        nib = np.empty((g, 128, n, 4), np.uint8)
        nib[..., 0::2] = words & 0xF
        nib[..., 1::2] = words >> 4
        vals = E2M1[nib]
    vals = vals * np.repeat(np.exp2(scales.astype(np.float64) - 127.0), 8, axis=1)[..., None]
    return vals.transpose(0, 1, 3, 2).reshape(g * 512, n)


B, N, T, D, NQ = 1, 512, 2048, 512, 128


def setup_inputs():
    n = np.random.standard_normal
    idx = np.random.permutation(T)[:B * N]
    s = mx_kscale(D)[:, None]
    kp = pack_weight(n((D, T)) / s, "e4m3")
    cp = pack_weight(n((D, T)) / s, "e4m3")
    return {
        "qT": (n((B, D, NQ)) * s * (1.00 / np.sqrt(D))).astype(np.float32),
        "k_words": kp[0],
        "k_scales": kp[1],
        "c_words": cp[0],
        "c_scales": cp[1],
        "ns": np.tile(np.random.uniform(0.2, 2.0, 2048), (128, 1)).astype(np.float32),
        "offs": striped(idx),
    }


def reference(qT, k_words, k_scales, c_words, c_scales, ns, offs):
    idx = unstriped(offs)
    pick = lambda x, which: x[:, which].reshape(x.shape[0], B, -1).transpose(1, 0, 2)
    k = unpack_weight(k_words, k_scales, "e4m3")
    kg = pick(k, idx)
    c = unpack_weight(c_words, c_scales, "e4m3")
    cg = pick(c, idx)
    qq = mxq(f64(qT), 1, "e4m3")
    a = qq.transpose(0, 2, 1) @ kg
    z = qq.transpose(0, 2, 1) @ cg
    y = a * z * pick(f64(ns), idx)[:, :1, :]
    return y

@@ -1,0 +1,126 @@
+from contextlib import ExitStack
+
+import concourse.mybir as mybir
+from concourse.masks import make_identity
+
+F32 = mybir.dt.float32
+BF16 = mybir.dt.bfloat16
+I32 = mybir.dt.int32
+U32 = mybir.dt.uint32
+U16 = mybir.dt.uint16
+U8 = mybir.dt.uint8
+FP8X4 = mybir.dt.float8_e4m3fn_x4
+MULT = mybir.AluOpType.mult
+
+P = 128
+PACK = 4
+D = P * PACK
+NQ = 128
+POOL = 2048
+LISTED = 512
+HALF = LISTED // 2
+PER_COLUMN = 16
+QUADRANT = 32
+NS_RUN = POOL // P
+PER_BANK = 4
+C_PLANE = 4
+
+FLOPS = 2 * 2 * D * NQ * LISTED
+
+
+def tile_attend_neu_bilin_topk_kernel(tc, qT, k_words, k_scales, c_words, c_scales, ns, offs, out):
+    nc = tc.nc
+    with ExitStack() as ctx:
+        held = ctx.enter_context(tc.tile_pool(name="held", bufs=1))
+        psum = ctx.enter_context(tc.psum_pool(name="psum", bufs=1))
+
+        offsets = held.tile([P, LISTED // PER_COLUMN], U16, name="offsets")
+        nc.sync.dma_start(offsets[:], offs)
+        ks_pool = held.tile([P, POOL // 4], I32, name="ks_pool", tag="ks_then_k", align_bytes=64)
+        nc.vector.memset(ks_pool[:], 0)
+        for r, queue in enumerate((nc.sync, nc.sync, nc.sync, nc.sync)):
+            queue.dma_start(ks_pool[r:P:QUADRANT, :], k_scales[0, r:16:4, :].bitcast(I32))
+        ns_runs = held.tile([P, NS_RUN], F32, name="ns_runs")
+        nc.scalar.dma_start(ns_runs[:], ns[0].rearrange("(p j) -> p j", j=NS_RUN))
+        q_raw = held.tile([P, PACK, NQ], F32, name="q_raw", tag="q_then_c")
+        nc.scalar.dma_start(q_raw[:], qT[0].rearrange("(p j) w -> p j w", j=PACK))
+        k_pool = held.tile([P, POOL], U32, name="k_pool", tag="k_then_cs", align_bytes=64)
+        nc.scalar.dma_start(k_pool[:].bitcast(I32), k_words[0].rearrange("p n t -> p (n t)").bitcast(I32))
+        cs_pool = held.tile([P, POOL // 4], I32, name="cs_pool")
+        nc.vector.memset(cs_pool[:], 0)
+        for r, queue in enumerate((nc.sync, nc.sync, nc.sync, nc.sync)):
+            queue.dma_start(cs_pool[C_PLANE + r : P : QUADRANT, :], c_scales[0, r:16:4, :].bitcast(I32))
+        identity = held.tile([P, P], F32, name="identity")
+        make_identity(nc, identity[:])
+
+        ks_listed = held.tile([P, LISTED], U8, name="ks_listed", align_bytes=64)
+        nc.vector.tensor_copy(ks_listed[:], ks_pool[:].bitcast(U8).indirect(offsets[:]))
+
+        q_grouped = held.tile([P, NQ, PACK], BF16, name="q_grouped", align_bytes=64)
+        nc.scalar.copy(q_grouped[:], q_raw[:].rearrange("p j w -> p w j"))
+        c_pool = held.tile([P, POOL], U32, name="c_pool", tag="q_then_c")
+        nc.scalar.dma_start(c_pool[:].bitcast(I32), c_words[0].rearrange("p n t -> p (n t)").bitcast(I32))
+        q_codes = held.tile([P, NQ], U32, name="q_codes", align_bytes=64)
+        q_scales = held.tile([P, NQ], U8, name="q_scales", align_bytes=64)
+        nc.vector.quantize_mx(
+            out=q_codes[:].bitcast(FP8X4), scales=q_scales[:], in_=q_grouped[:].rearrange("p w j -> p (w j)")
+        )
+
+        ns_pool = held.tile([P, POOL], F32, name="ns_pool")
+        ns_by_run = ns_pool[:].rearrange("q (p j) -> q p j", j=NS_RUN)
+        for b in range(NS_RUN // PER_BANK):
+            spread = psum.tile([P, PER_BANK, P], F32, name=f"spread{b}", tag=f"bank{b}")
+            for j in range(PER_BANK):
+                column = b * PER_BANK + j
+                nc.tensor.transpose(
+                    spread[:, j, :], ns_runs[:, column : column + 1].to_broadcast([P, P]), identity[:]
+                )
+            nc.scalar.copy(
+                ns_by_run[:, :, b * PER_BANK : (b + 1) * PER_BANK], spread[:].rearrange("q j p -> q p j")
+            )
+
+        k_listed = held.tile([P, LISTED], U32, name="k_listed", tag="ks_then_k", align_bytes=64)
+        nc.vector.tensor_copy(k_listed[:], k_pool[:].indirect(offsets[:]))
+        gate = psum.tile([NQ, LISTED], F32, name="gate", tag="bank0")
+        nc.tensor.matmul_mx(
+            out=gate[:],
+            lhsT=q_codes[:].bitcast(FP8X4),
+            lhsT_scale=q_scales[:],
+            rhs=k_listed[:].bitcast(FP8X4),
+            rhs_scale=ks_listed[:],
+            start=True,
+            stop=True,
+        )
+        gate_sb = held.tile([NQ, LISTED], F32, name="gate_sb")
+        nc.scalar.copy(gate_sb[:], gate[:])
+
+        cs_listed = held.tile([P, LISTED], U8, name="cs_listed", tag="k_then_cs", align_bytes=64)
+        nc.vector.tensor_copy(cs_listed[:], cs_pool[:].bitcast(U8).indirect(offsets[:]))
+        c_listed = held.tile([P, LISTED], U32, name="c_listed", align_bytes=64)
+        nc.vector.tensor_copy(c_listed[:], c_pool[:].indirect(offsets[:]))
+
+        halves = [slice(h * HALF, (h + 1) * HALF) for h in range(2)]
+        layer = []
+        scaled = []
+        for h, cols in enumerate(halves):
+            bank = psum.tile([NQ, HALF], F32, name=f"layer{h}")
+            nc.tensor.matmul_mx(
+                out=bank[:],
+                lhsT=q_codes[:].bitcast(FP8X4),
+                lhsT_scale=q_scales[:],
+                rhs=c_listed[:, cols].bitcast(FP8X4),
+                rhs_scale=cs_listed[C_PLANE:P, cols],
+                start=True,
+                stop=True,
+            )
+            layer.append(bank)
+        for h, cols in enumerate(halves):
+            part = held.tile([NQ, HALF], F32, name=f"scaled{h}")
+            entries = offsets[:, h * HALF // PER_COLUMN : (h + 1) * HALF // PER_COLUMN]
+            nc.vector.tensor_tensor(part[:], ns_pool[:].indirect(entries), gate_sb[:, cols], MULT)
+            scaled.append(part)
+        for h, cols in enumerate(halves):
+            result = held.tile([NQ, HALF], F32, name=f"result{h}")
+            nc.vector.tensor_tensor(result[:], layer[h][:], scaled[h][:], MULT)
+            queue = nc.sync if h == 0 else nc.scalar
+            queue.dma_start(out[0, :, cols], result[:])

@@ -1,7 +1,6 @@
 from contextlib import ExitStack
 
 import concourse.mybir as mybir
-from concourse.masks import make_identity
 
 F32 = mybir.dt.float32
 BF16 = mybir.dt.bfloat16
@@ -24,6 +23,11 @@ QUADRANT = 32
 NS_RUN = POOL // P
 PER_BANK = 4
 C_PLANE = 4
+K_END = 4 * POOL
+CS_END = K_END + POOL
+KS_END = CS_END + LISTED
+Q_END = KS_END + 2 * D
+C_END = Q_END + 4 * POOL
 
 FLOPS = 2 * 2 * D * NQ * LISTED
 
@@ -34,32 +38,42 @@ def tile_attend_neu_bilin_topk_kernel(tc, qT, k_words, k_scales, c_words, c_scal
         held = ctx.enter_context(tc.tile_pool(name="held", bufs=1))
         psum = ctx.enter_context(tc.psum_pool(name="psum", bufs=1))
 
+        placed = ctx.enter_context(tc.tile_pool(name="placed", bufs=1))
+
         offsets = held.tile([P, LISTED // PER_COLUMN], U16, name="offsets")
         nc.sync.dma_start(offsets[:], offs)
         ks_pool = held.tile([P, POOL // 4], I32, name="ks_pool", tag="ks_then_k", align_bytes=64)
         nc.vector.memset(ks_pool[:], 0)
-        for r, queue in enumerate((nc.sync, nc.sync, nc.sync, nc.sync)):
-            queue.dma_start(ks_pool[r:P:QUADRANT, :], k_scales[0, r:16:4, :].bitcast(I32))
+        for r in range(4):
+            nc.sync.dma_start(ks_pool[r:P:QUADRANT, :], k_scales[0, r:16:4, :].bitcast(I32))
         ns_runs = held.tile([P, NS_RUN], F32, name="ns_runs")
         nc.scalar.dma_start(ns_runs[:], ns[0].rearrange("(p j) -> p j", j=NS_RUN))
-        q_raw = held.tile([P, PACK, NQ], F32, name="q_raw", tag="q_then_c")
+        q_raw = placed.tile([P, PACK, NQ], F32, name="q_raw", offset=Q_END)
         nc.scalar.dma_start(q_raw[:], qT[0].rearrange("(p j) w -> p j w", j=PACK))
-        k_pool = held.tile([P, POOL], U32, name="k_pool", tag="k_then_cs", align_bytes=64)
-        nc.scalar.dma_start(k_pool[:].bitcast(I32), k_words[0].rearrange("p n t -> p (n t)").bitcast(I32))
-        cs_pool = held.tile([P, POOL // 4], I32, name="cs_pool")
-        nc.vector.memset(cs_pool[:], 0)
-        for r, queue in enumerate((nc.sync, nc.sync, nc.sync, nc.sync)):
-            queue.dma_start(cs_pool[C_PLANE + r : P : QUADRANT, :], c_scales[0, r:16:4, :].bitcast(I32))
-        identity = held.tile([P, P], F32, name="identity")
-        make_identity(nc, identity[:])
 
-        ks_listed = held.tile([P, LISTED], U8, name="ks_listed", align_bytes=64)
+        identity = held.tile([P, P], F32, name="identity")
+        left = placed.tile([P, P // 2], I32, name="left", offset=K_END - P)
+        right = placed.tile([P, P // 2], I32, name="right", offset=KS_END - P)
+        nc.gpsimd.iota(left[:], [[1, P // 2]], base=0, channel_multiplier=-1)
+        nc.gpsimd.iota(right[:], [[1, P // 2]], base=P // 2, channel_multiplier=-1)
+        nc.vector.tensor_scalar(identity[:, : P // 2], left[:], 0.0, None, mybir.AluOpType.is_equal)
+
+        k_pool = placed.tile([P, POOL], U32, name="k_pool", offset=0)
+        nc.sync.dma_start(k_pool[:].bitcast(I32), k_words[0].rearrange("p n t -> p (n t)").bitcast(I32))
+        cs_pool = placed.tile([P, POOL // 4], I32, name="cs_pool", offset=K_END)
+        nc.vector.memset(cs_pool[:], 0)
+        for r in range(4):
+            nc.sync.dma_start(cs_pool[C_PLANE + r : P : QUADRANT, :], c_scales[0, r:16:4, :].bitcast(I32))
+        nc.vector.tensor_scalar(identity[:, P // 2 :], right[:], 0.0, None, mybir.AluOpType.is_equal)
+
+        q_grouped = placed.tile([P, NQ, PACK], BF16, name="q_grouped", offset=KS_END, align_bytes=64)
+        nc.vector.tensor_copy(q_grouped[:], q_raw[:].rearrange("p j w -> p w j"))
+        c_pool = placed.tile([P, POOL], U32, name="c_pool", offset=Q_END)
+        nc.sync.dma_start(c_pool[:].bitcast(I32), c_words[0].rearrange("p n t -> p (n t)").bitcast(I32))
+
+        ks_listed = placed.tile([P, LISTED], U8, name="ks_listed", offset=CS_END, align_bytes=64)
         nc.vector.tensor_copy(ks_listed[:], ks_pool[:].bitcast(U8).indirect(offsets[:]))
 
-        q_grouped = held.tile([P, NQ, PACK], BF16, name="q_grouped", align_bytes=64)
-        nc.scalar.copy(q_grouped[:], q_raw[:].rearrange("p j w -> p w j"))
-        c_pool = held.tile([P, POOL], U32, name="c_pool", tag="q_then_c")
-        nc.scalar.dma_start(c_pool[:].bitcast(I32), c_words[0].rearrange("p n t -> p (n t)").bitcast(I32))
         q_codes = held.tile([P, NQ], U32, name="q_codes", align_bytes=64)
         q_scales = held.tile([P, NQ], U8, name="q_scales", align_bytes=64)
         nc.vector.quantize_mx(
@@ -94,30 +108,32 @@ def tile_attend_neu_bilin_topk_kernel(tc, qT, k_words, k_scales, c_words, c_scal
         gate_sb = held.tile([NQ, LISTED], F32, name="gate_sb")
         nc.scalar.copy(gate_sb[:], gate[:])
 
-        cs_listed = held.tile([P, LISTED], U8, name="cs_listed", tag="k_then_cs", align_bytes=64)
+        cs_listed = held.tile([P, LISTED], U8, name="cs_listed", align_bytes=64)
         nc.vector.tensor_copy(cs_listed[:], cs_pool[:].bitcast(U8).indirect(offsets[:]))
-        c_listed = held.tile([P, LISTED], U32, name="c_listed", align_bytes=64)
-        nc.vector.tensor_copy(c_listed[:], c_pool[:].indirect(offsets[:]))
 
         halves = [slice(h * HALF, (h + 1) * HALF) for h in range(2)]
+        entries = [offsets[:, h * HALF // PER_COLUMN : (h + 1) * HALF // PER_COLUMN] for h in range(2)]
         layer = []
         scaled = []
         for h, cols in enumerate(halves):
+            c_listed = placed.tile(
+                [P, HALF], U32, name=f"c_listed{h}", offset=C_END + (2 * HALF, 8 * HALF)[h], align_bytes=64
+            )
+            nc.vector.tensor_copy(c_listed[:], c_pool[:].indirect(entries[h]))
             bank = psum.tile([NQ, HALF], F32, name=f"layer{h}")
             nc.tensor.matmul_mx(
                 out=bank[:],
                 lhsT=q_codes[:].bitcast(FP8X4),
                 lhsT_scale=q_scales[:],
-                rhs=c_listed[:, cols].bitcast(FP8X4),
+                rhs=c_listed[:].bitcast(FP8X4),
                 rhs_scale=cs_listed[C_PLANE:P, cols],
                 start=True,
                 stop=True,
             )
             layer.append(bank)
         for h, cols in enumerate(halves):
-            part = held.tile([NQ, HALF], F32, name=f"scaled{h}")
-            entries = offsets[:, h * HALF // PER_COLUMN : (h + 1) * HALF // PER_COLUMN]
-            nc.vector.tensor_tensor(part[:], ns_pool[:].indirect(entries), gate_sb[:, cols], MULT)
+            part = placed.tile([NQ, HALF], F32, name=f"scaled{h}", offset=C_END + 4 * HALF * h)
+            nc.vector.tensor_tensor(part[:], ns_pool[:].indirect(entries[h]), gate_sb[:, cols], MULT)
             scaled.append(part)
         for h, cols in enumerate(halves):
             result = held.tile([NQ, HALF], F32, name=f"result{h}")

@@ -27,7 +27,6 @@ K_END = 4 * POOL
 CS_END = K_END + POOL
 KS_END = CS_END + LISTED
 Q_END = KS_END + 2 * D
-C_END = Q_END + 4 * POOL
 
 FLOPS = 2 * 2 * D * NQ * LISTED
 
@@ -44,8 +43,8 @@ def tile_attend_neu_bilin_topk_kernel(tc, qT, k_words, k_scales, c_words, c_scal
         nc.sync.dma_start(offsets[:], offs)
         ks_pool = held.tile([P, POOL // 4], I32, name="ks_pool", tag="ks_then_k", align_bytes=64)
         nc.vector.memset(ks_pool[:], 0)
-        for r in range(4):
-            nc.sync.dma_start(ks_pool[r:P:QUADRANT, :], k_scales[0, r:16:4, :].bitcast(I32))
+        for r, queue in enumerate((nc.sync, nc.scalar, nc.sync, nc.scalar)):
+            queue.dma_start(ks_pool[r:P:QUADRANT, :], k_scales[0, r:16:4, :].bitcast(I32))
         ns_runs = held.tile([P, NS_RUN], F32, name="ns_runs")
         nc.scalar.dma_start(ns_runs[:], ns[0].rearrange("(p j) -> p j", j=NS_RUN))
         q_raw = placed.tile([P, PACK, NQ], F32, name="q_raw", offset=Q_END)
@@ -63,7 +62,7 @@ def tile_attend_neu_bilin_topk_kernel(tc, qT, k_words, k_scales, c_words, c_scal
         cs_pool = placed.tile([P, POOL // 4], I32, name="cs_pool", offset=K_END)
         nc.vector.memset(cs_pool[:], 0)
         for r in range(4):
-            nc.sync.dma_start(cs_pool[C_PLANE + r : P : QUADRANT, :], c_scales[0, r:16:4, :].bitcast(I32))
+            nc.scalar.dma_start(cs_pool[C_PLANE + r : P : QUADRANT, :], c_scales[0, r:16:4, :].bitcast(I32))
         nc.vector.tensor_scalar(identity[:, P // 2 :], right[:], 0.0, None, mybir.AluOpType.is_equal)
 
         q_grouped = placed.tile([P, NQ, PACK], BF16, name="q_grouped", offset=KS_END, align_bytes=64)
@@ -93,48 +92,46 @@ def tile_attend_neu_bilin_topk_kernel(tc, qT, k_words, k_scales, c_words, c_scal
                 ns_by_run[:, :, b * PER_BANK : (b + 1) * PER_BANK], spread[:].rearrange("q j p -> q p j")
             )
 
-        k_listed = held.tile([P, LISTED], U32, name="k_listed", tag="ks_then_k", align_bytes=64)
-        nc.vector.tensor_copy(k_listed[:], k_pool[:].indirect(offsets[:]))
-        gate = psum.tile([NQ, LISTED], F32, name="gate", tag="bank0")
-        nc.tensor.matmul_mx(
-            out=gate[:],
-            lhsT=q_codes[:].bitcast(FP8X4),
-            lhsT_scale=q_scales[:],
-            rhs=k_listed[:].bitcast(FP8X4),
-            rhs_scale=ks_listed[:],
-            start=True,
-            stop=True,
-        )
-        gate_sb = held.tile([NQ, LISTED], F32, name="gate_sb")
-        nc.scalar.copy(gate_sb[:], gate[:])
-
-        cs_listed = held.tile([P, LISTED], U8, name="cs_listed", align_bytes=64)
-        nc.vector.tensor_copy(cs_listed[:], cs_pool[:].bitcast(U8).indirect(offsets[:]))
-
         halves = [slice(h * HALF, (h + 1) * HALF) for h in range(2)]
         entries = [offsets[:, h * HALF // PER_COLUMN : (h + 1) * HALF // PER_COLUMN] for h in range(2)]
-        layer = []
-        scaled = []
-        for h, cols in enumerate(halves):
-            c_listed = placed.tile(
-                [P, HALF], U32, name=f"c_listed{h}", offset=C_END + (2 * HALF, 8 * HALF)[h], align_bytes=64
-            )
-            nc.vector.tensor_copy(c_listed[:], c_pool[:].indirect(entries[h]))
-            bank = psum.tile([NQ, HALF], F32, name=f"layer{h}")
+
+        def product(name, tag, codes, scales):
+            bank = psum.tile([NQ, HALF], F32, name=name, tag=tag)
             nc.tensor.matmul_mx(
                 out=bank[:],
                 lhsT=q_codes[:].bitcast(FP8X4),
                 lhsT_scale=q_scales[:],
-                rhs=c_listed[:].bitcast(FP8X4),
-                rhs_scale=cs_listed[C_PLANE:P, cols],
+                rhs=codes.bitcast(FP8X4),
+                rhs_scale=scales,
                 start=True,
                 stop=True,
             )
-            layer.append(bank)
+            return bank
+
+        k_listed = held.tile([P, LISTED], U32, name="k_listed", tag="ks_then_k", align_bytes=64)
+        nc.vector.tensor_copy(k_listed[:], k_pool[:].indirect(offsets[:]))
+        gate = []
         for h, cols in enumerate(halves):
-            part = placed.tile([NQ, HALF], F32, name=f"scaled{h}", offset=C_END + 4 * HALF * h)
-            nc.vector.tensor_tensor(part[:], ns_pool[:].indirect(entries[h]), gate_sb[:, cols], MULT)
-            scaled.append(part)
+            bank = product(f"gate{h}", f"bank{h}", k_listed[:, cols], ks_listed[:, cols])
+            copied = held.tile([NQ, HALF], F32, name=f"gate_sb{h}")
+            nc.scalar.copy(copied[:], bank[:])
+            gate.append(copied)
+
+        cs_listed = held.tile([P, LISTED], U8, name="cs_listed", align_bytes=64)
+        nc.vector.tensor_copy(cs_listed[:], cs_pool[:].bitcast(U8).indirect(offsets[:]))
+
+        def scale(h):
+            part = held.tile([NQ, HALF], F32, name=f"scaled{h}")
+            nc.vector.tensor_tensor(part[:], ns_pool[:].indirect(entries[h]), gate[h][:], MULT)
+            return part
+
+        scaled = [scale(0)]
+        layer = []
+        for h, cols in enumerate(halves):
+            c_listed = held.tile([P, HALF], U32, name=f"c_listed{h}", align_bytes=64)
+            nc.vector.tensor_copy(c_listed[:], c_pool[:].indirect(entries[h]))
+            layer.append(product(f"layer{h}", f"layer{h}", c_listed[:], cs_listed[C_PLANE:P, cols]))
+        scaled.append(scale(1))
         for h, cols in enumerate(halves):
             result = held.tile([NQ, HALF], F32, name=f"result{h}")
             nc.vector.tensor_tensor(result[:], layer[h][:], scaled[h][:], MULT)

@@ -1,6 +1,7 @@
 from contextlib import ExitStack
 
 import concourse.mybir as mybir
+from concourse.masks import make_identity
 
 F32 = mybir.dt.float32
 BF16 = mybir.dt.bfloat16
@@ -10,6 +11,7 @@ U16 = mybir.dt.uint16
 U8 = mybir.dt.uint8
 FP8X4 = mybir.dt.float8_e4m3fn_x4
 MULT = mybir.AluOpType.mult
+COPY = mybir.ActivationFunctionType.Copy
 
 P = 128
 PACK = 4
@@ -18,15 +20,11 @@ NQ = 128
 POOL = 2048
 LISTED = 512
 HALF = LISTED // 2
+BLOCKS = LISTED // P
 PER_COLUMN = 16
 QUADRANT = 32
-NS_RUN = POOL // P
-PER_BANK = 4
+NS_ROW = P - 1
 C_PLANE = 4
-K_END = 4 * POOL
-CS_END = K_END + POOL
-KS_END = CS_END + LISTED
-Q_END = KS_END + 2 * D
 
 FLOPS = 2 * 2 * D * NQ * LISTED
 
@@ -37,40 +35,43 @@ def tile_attend_neu_bilin_topk_kernel(tc, qT, k_words, k_scales, c_words, c_scal
         held = ctx.enter_context(tc.tile_pool(name="held", bufs=1))
         psum = ctx.enter_context(tc.psum_pool(name="psum", bufs=1))
 
-        placed = ctx.enter_context(tc.tile_pool(name="placed", bufs=1))
-
         offsets = held.tile([P, LISTED // PER_COLUMN], U16, name="offsets")
         nc.sync.dma_start(offsets[:], offs)
-        ks_pool = held.tile([P, POOL // 4], I32, name="ks_pool", tag="ks_then_k", align_bytes=64)
+        ns_pool = held.tile([P, POOL], F32, name="ns_pool")
+        nc.sync.dma_start(ns_pool[NS_ROW:P, :], ns[0:1, :])
+        q_raw = held.tile([P, PACK, NQ], F32, name="q_raw")
+        nc.sync.dma_start(q_raw[:], qT[0].rearrange("(p j) w -> p j w", j=PACK))
+
+        ks_pool = held.tile([P, POOL // 4], I32, name="ks_pool")
         nc.vector.memset(ks_pool[:], 0)
-        for r, queue in enumerate((nc.sync, nc.scalar, nc.sync, nc.scalar)):
-            queue.dma_start(ks_pool[r:P:QUADRANT, :], k_scales[0, r:16:4, :].bitcast(I32))
-        ns_runs = held.tile([P, NS_RUN], F32, name="ns_runs")
-        nc.scalar.dma_start(ns_runs[:], ns[0].rearrange("(p j) -> p j", j=NS_RUN))
-        q_raw = placed.tile([P, PACK, NQ], F32, name="q_raw", offset=Q_END)
-        nc.scalar.dma_start(q_raw[:], qT[0].rearrange("(p j) w -> p j w", j=PACK))
+        for r in range(4):
+            nc.sync.dma_start(ks_pool[r:P:QUADRANT, :], k_scales[0, r:16:4, :].bitcast(I32))
 
         identity = held.tile([P, P], F32, name="identity")
-        left = placed.tile([P, P // 2], I32, name="left", offset=K_END - P)
-        right = placed.tile([P, P // 2], I32, name="right", offset=KS_END - P)
-        nc.gpsimd.iota(left[:], [[1, P // 2]], base=0, channel_multiplier=-1)
-        nc.gpsimd.iota(right[:], [[1, P // 2]], base=P // 2, channel_multiplier=-1)
-        nc.vector.tensor_scalar(identity[:, : P // 2], left[:], 0.0, None, mybir.AluOpType.is_equal)
+        make_identity(nc, identity[:])
 
-        k_pool = placed.tile([P, POOL], U32, name="k_pool", offset=0)
+        k_pool = held.tile([P, POOL], U32, name="k_pool")
         nc.sync.dma_start(k_pool[:].bitcast(I32), k_words[0].rearrange("p n t -> p (n t)").bitcast(I32))
-        cs_pool = placed.tile([P, POOL // 4], I32, name="cs_pool", offset=K_END)
+        nc.vector.memset(ns_pool[:NS_ROW, :], 0.0)
+        cs_pool = held.tile([P, POOL // 4], I32, name="cs_pool")
         nc.vector.memset(cs_pool[:], 0)
         for r in range(4):
-            nc.scalar.dma_start(cs_pool[C_PLANE + r : P : QUADRANT, :], c_scales[0, r:16:4, :].bitcast(I32))
-        nc.vector.tensor_scalar(identity[:, P // 2 :], right[:], 0.0, None, mybir.AluOpType.is_equal)
-
-        q_grouped = placed.tile([P, NQ, PACK], BF16, name="q_grouped", offset=KS_END, align_bytes=64)
-        nc.vector.tensor_copy(q_grouped[:], q_raw[:].rearrange("p j w -> p w j"))
-        c_pool = placed.tile([P, POOL], U32, name="c_pool", offset=Q_END)
+            nc.sync.dma_start(cs_pool[C_PLANE + r : P : QUADRANT, :], c_scales[0, r:16:4, :].bitcast(I32))
+        c_pool = held.tile([P, POOL], U32, name="c_pool")
         nc.sync.dma_start(c_pool[:].bitcast(I32), c_words[0].rearrange("p n t -> p (n t)").bitcast(I32))
 
-        ks_listed = placed.tile([P, LISTED], U8, name="ks_listed", offset=CS_END, align_bytes=64)
+        ns_listed = held.tile([P, LISTED], F32, name="ns_listed")
+        nc.vector.tensor_copy(ns_listed[:], ns_pool[:].indirect(offsets[:]))
+        ns_turned = psum.tile([P, BLOCKS, P], F32, name="ns_turned", tag="bank0")
+        for b in range(BLOCKS):
+            nc.tensor.transpose(ns_turned[:, b, :], ns_listed[:, b * P : (b + 1) * P], identity[:])
+
+        q_grouped = held.tile([P, NQ, PACK], BF16, name="q_grouped", align_bytes=64)
+        nc.scalar.copy(q_grouped[:], q_raw[:].rearrange("p j w -> p w j"))
+        ns_columns = held.tile([P, BLOCKS], F32, name="ns_columns")
+        nc.scalar.copy(ns_columns[:], ns_turned[:, :, NS_ROW])
+
+        ks_listed = held.tile([P, LISTED], U8, name="ks_listed", align_bytes=64)
         nc.vector.tensor_copy(ks_listed[:], ks_pool[:].bitcast(U8).indirect(offsets[:]))
 
         q_codes = held.tile([P, NQ], U32, name="q_codes", align_bytes=64)
@@ -79,61 +80,56 @@ def tile_attend_neu_bilin_topk_kernel(tc, qT, k_words, k_scales, c_words, c_scal
             out=q_codes[:].bitcast(FP8X4), scales=q_scales[:], in_=q_grouped[:].rearrange("p w j -> p (w j)")
         )
 
-        ns_pool = held.tile([P, POOL], F32, name="ns_pool")
-        ns_by_run = ns_pool[:].rearrange("q (p j) -> q p j", j=NS_RUN)
-        for b in range(NS_RUN // PER_BANK):
-            spread = psum.tile([P, PER_BANK, P], F32, name=f"spread{b}", tag=f"bank{b}")
-            for j in range(PER_BANK):
-                column = b * PER_BANK + j
-                nc.tensor.transpose(
-                    spread[:, j, :], ns_runs[:, column : column + 1].to_broadcast([P, P]), identity[:]
-                )
-            nc.scalar.copy(
-                ns_by_run[:, :, b * PER_BANK : (b + 1) * PER_BANK], spread[:].rearrange("q j p -> q p j")
-            )
-
         halves = [slice(h * HALF, (h + 1) * HALF) for h in range(2)]
         entries = [offsets[:, h * HALF // PER_COLUMN : (h + 1) * HALF // PER_COLUMN] for h in range(2)]
 
-        def product(name, tag, codes, scales):
-            bank = psum.tile([NQ, HALF], F32, name=name, tag=tag)
-            nc.tensor.matmul_mx(
-                out=bank[:],
-                lhsT=q_codes[:].bitcast(FP8X4),
-                lhsT_scale=q_scales[:],
-                rhs=codes.bitcast(FP8X4),
-                rhs_scale=scales,
-                start=True,
-                stop=True,
-            )
-            return bank
-
-        k_listed = held.tile([P, LISTED], U32, name="k_listed", tag="ks_then_k", align_bytes=64)
-        nc.vector.tensor_copy(k_listed[:], k_pool[:].indirect(offsets[:]))
         gate = []
-        for h, cols in enumerate(halves):
-            bank = product(f"gate{h}", f"bank{h}", k_listed[:, cols], ks_listed[:, cols])
-            copied = held.tile([NQ, HALF], F32, name=f"gate_sb{h}")
-            nc.scalar.copy(copied[:], bank[:])
+        for h in range(2):
+            k_listed = held.tile([P, HALF], U32, name=f"k_listed{h}", align_bytes=64)
+            nc.vector.tensor_copy(k_listed[:], k_pool[:].indirect(entries[h]))
+            by_slot = psum.tile([P, 2, NQ], F32, name=f"by_slot{h}", tag=f"bank{h}")
+            for j in range(2):
+                b = 2 * h + j
+                nc.tensor.matmul_mx(
+                    out=by_slot[:, j, :],
+                    lhsT=k_listed[:, j * P : (j + 1) * P].bitcast(FP8X4),
+                    lhsT_scale=ks_listed[:, b * P : (b + 1) * P],
+                    rhs=q_codes[:].bitcast(FP8X4),
+                    rhs_scale=q_scales[:],
+                    start=True,
+                    stop=True,
+                )
+            scaled = held.tile([P, 2, NQ], F32, name=f"scaled{h}")
+            by_query = psum.tile([NQ, 2, P], F32, name=f"by_query{h}")
+            for j in range(2):
+                b = 2 * h + j
+                nc.scalar.activation(scaled[:, j, :], by_slot[:, j, :], COPY, scale=ns_columns[:, b : b + 1])
+            for j in range(2):
+                nc.tensor.transpose(by_query[:, j, :], scaled[:, j, :], identity[:])
+            copied = held.tile([NQ, HALF], F32, name=f"gate{h}")
+            nc.scalar.copy(copied[:], by_query[:].rearrange("q j p -> q (j p)"))
             gate.append(copied)
 
         cs_listed = held.tile([P, LISTED], U8, name="cs_listed", align_bytes=64)
         nc.vector.tensor_copy(cs_listed[:], cs_pool[:].bitcast(U8).indirect(offsets[:]))
 
-        def scale(h):
-            part = held.tile([NQ, HALF], F32, name=f"scaled{h}")
-            nc.vector.tensor_tensor(part[:], ns_pool[:].indirect(entries[h]), gate[h][:], MULT)
-            return part
-
-        scaled = [scale(0)]
         layer = []
         for h, cols in enumerate(halves):
             c_listed = held.tile([P, HALF], U32, name=f"c_listed{h}", align_bytes=64)
             nc.vector.tensor_copy(c_listed[:], c_pool[:].indirect(entries[h]))
-            layer.append(product(f"layer{h}", f"layer{h}", c_listed[:], cs_listed[C_PLANE:P, cols]))
-        scaled.append(scale(1))
+            bank = psum.tile([NQ, HALF], F32, name=f"layer{h}")
+            nc.tensor.matmul_mx(
+                out=bank[:],
+                lhsT=q_codes[:].bitcast(FP8X4),
+                lhsT_scale=q_scales[:],
+                rhs=c_listed[:].bitcast(FP8X4),
+                rhs_scale=cs_listed[C_PLANE:P, cols],
+                start=True,
+                stop=True,
+            )
+            layer.append(bank)
         for h, cols in enumerate(halves):
             result = held.tile([NQ, HALF], F32, name=f"result{h}")
-            nc.vector.tensor_tensor(result[:], layer[h][:], scaled[h][:], MULT)
+            nc.vector.tensor_tensor(result[:], layer[h][:], gate[h][:], MULT)
             queue = nc.sync if h == 0 else nc.scalar
             queue.dma_start(out[0, :, cols], result[:])

@@ -70,6 +70,11 @@ def tile_attend_neu_bilin_topk_kernel(tc, qT, k_words, k_scales, c_words, c_scal
         nc.scalar.copy(q_grouped[:], q_raw[:].rearrange("p j w -> p w j"))
         ns_columns = held.tile([P, BLOCKS], F32, name="ns_columns")
         nc.scalar.copy(ns_columns[:], ns_turned[:, :, NS_ROW])
+        ns_spread = psum.tile([NQ, 2, P], F32, name="ns_spread")
+        for j in range(2):
+            nc.tensor.transpose(ns_spread[:, j, :], ns_columns[:, 2 + j : 3 + j].to_broadcast([P, P]), identity[:])
+        ns_rows = held.tile([NQ, HALF], F32, name="ns_rows")
+        nc.scalar.copy(ns_rows[:], ns_spread[:].rearrange("q j p -> q (j p)"))
 
         ks_listed = held.tile([P, LISTED], U8, name="ks_listed", align_bytes=64)
         nc.vector.tensor_copy(ks_listed[:], ks_pool[:].bitcast(U8).indirect(offsets[:]))
@@ -83,53 +88,59 @@ def tile_attend_neu_bilin_topk_kernel(tc, qT, k_words, k_scales, c_words, c_scal
         halves = [slice(h * HALF, (h + 1) * HALF) for h in range(2)]
         entries = [offsets[:, h * HALF // PER_COLUMN : (h + 1) * HALF // PER_COLUMN] for h in range(2)]
 
-        gate = []
+        def by_query_product(name, codes, scales):
+            bank = psum.tile([NQ, HALF], F32, name=name)
+            nc.tensor.matmul_mx(
+                out=bank[:],
+                lhsT=q_codes[:].bitcast(FP8X4),
+                lhsT_scale=q_scales[:],
+                rhs=codes.bitcast(FP8X4),
+                rhs_scale=scales,
+                start=True,
+                stop=True,
+            )
+            return bank
+
+        k_listed = []
         for h in range(2):
-            k_listed = held.tile([P, HALF], U32, name=f"k_listed{h}", align_bytes=64)
-            nc.vector.tensor_copy(k_listed[:], k_pool[:].indirect(entries[h]))
-            by_slot = psum.tile([P, 2, NQ], F32, name=f"by_slot{h}", tag=f"bank{h}")
-            for j in range(2):
-                b = 2 * h + j
-                nc.tensor.matmul_mx(
-                    out=by_slot[:, j, :],
-                    lhsT=k_listed[:, j * P : (j + 1) * P].bitcast(FP8X4),
-                    lhsT_scale=ks_listed[:, b * P : (b + 1) * P],
-                    rhs=q_codes[:].bitcast(FP8X4),
-                    rhs_scale=q_scales[:],
-                    start=True,
-                    stop=True,
-                )
-            scaled = held.tile([P, 2, NQ], F32, name=f"scaled{h}")
-            by_query = psum.tile([NQ, 2, P], F32, name=f"by_query{h}")
-            for j in range(2):
-                b = 2 * h + j
-                nc.scalar.activation(scaled[:, j, :], by_slot[:, j, :], COPY, scale=ns_columns[:, b : b + 1])
-            for j in range(2):
-                nc.tensor.transpose(by_query[:, j, :], scaled[:, j, :], identity[:])
-            copied = held.tile([NQ, HALF], F32, name=f"gate{h}")
-            nc.scalar.copy(copied[:], by_query[:].rearrange("q j p -> q (j p)"))
-            gate.append(copied)
+            listed = held.tile([P, HALF], U32, name=f"k_listed{h}", align_bytes=64)
+            nc.vector.tensor_copy(listed[:], k_pool[:].indirect(entries[h]))
+            k_listed.append(listed)
+
+        by_slot = psum.tile([P, 2, NQ], F32, name="by_slot", tag="bank0")
+        for j in range(2):
+            nc.tensor.matmul_mx(
+                out=by_slot[:, j, :],
+                lhsT=k_listed[0][:, j * P : (j + 1) * P].bitcast(FP8X4),
+                lhsT_scale=ks_listed[:, j * P : (j + 1) * P],
+                rhs=q_codes[:].bitcast(FP8X4),
+                rhs_scale=q_scales[:],
+                start=True,
+                stop=True,
+            )
+        gate1 = by_query_product("gate1", k_listed[1][:], ks_listed[:, halves[1]])
+        scaled_by_slot = held.tile([P, 2, NQ], F32, name="scaled_by_slot")
+        by_query = psum.tile([NQ, 2, P], F32, name="by_query")
+        for j in range(2):
+            nc.scalar.activation(scaled_by_slot[:, j, :], by_slot[:, j, :], COPY, scale=ns_columns[:, j : j + 1])
+        for j in range(2):
+            nc.tensor.transpose(by_query[:, j, :], scaled_by_slot[:, j, :], identity[:])
+        scaled0 = held.tile([NQ, HALF], F32, name="scaled0")
+        nc.scalar.copy(scaled0[:], by_query[:].rearrange("q j p -> q (j p)"))
 
         cs_listed = held.tile([P, LISTED], U8, name="cs_listed", align_bytes=64)
         nc.vector.tensor_copy(cs_listed[:], cs_pool[:].bitcast(U8).indirect(offsets[:]))
 
         layer = []
         for h, cols in enumerate(halves):
-            c_listed = held.tile([P, HALF], U32, name=f"c_listed{h}", align_bytes=64)
+            c_listed = held.tile([P, HALF], U32, name=f"c_listed{h}", tag=f"c_listed{h}", align_bytes=64)
             nc.vector.tensor_copy(c_listed[:], c_pool[:].indirect(entries[h]))
-            bank = psum.tile([NQ, HALF], F32, name=f"layer{h}")
-            nc.tensor.matmul_mx(
-                out=bank[:],
-                lhsT=q_codes[:].bitcast(FP8X4),
-                lhsT_scale=q_scales[:],
-                rhs=c_listed[:].bitcast(FP8X4),
-                rhs_scale=cs_listed[C_PLANE:P, cols],
-                start=True,
-                stop=True,
-            )
-            layer.append(bank)
+            layer.append(by_query_product(f"layer{h}", c_listed[:], cs_listed[C_PLANE:P, cols]))
+        scaled1 = held.tile([NQ, HALF], F32, name="scaled1", tag="c_listed0", align_bytes=64)
+        nc.vector.tensor_tensor(scaled1[:], gate1[:], ns_rows[:], MULT)
+        scaled = [scaled0, scaled1]
         for h, cols in enumerate(halves):
             result = held.tile([NQ, HALF], F32, name=f"result{h}")
-            nc.vector.tensor_tensor(result[:], layer[h][:], gate[h][:], MULT)
+            nc.vector.tensor_tensor(result[:], layer[h][:], scaled[h][:], MULT)
             queue = nc.sync if h == 0 else nc.scalar
             queue.dma_start(out[0, :, cols], result[:])

@@ -25,6 +25,7 @@ PER_COLUMN = 16
 QUADRANT = 32
 NS_ROW = P - 1
 C_PLANE = 4
+C_AHEAD = 768
 
 FLOPS = 2 * 2 * D * NQ * LISTED
 
@@ -53,12 +54,14 @@ def tile_attend_neu_bilin_topk_kernel(tc, qT, k_words, k_scales, c_words, c_scal
         k_pool = held.tile([P, POOL], U32, name="k_pool")
         nc.sync.dma_start(k_pool[:].bitcast(I32), k_words[0].rearrange("p n t -> p (n t)").bitcast(I32))
         nc.vector.memset(ns_pool[:NS_ROW, :], 0.0)
+        c_pool = held.tile([P, POOL], U32, name="c_pool")
+        c_dram = c_words[0].rearrange("p n t -> p (n t)").bitcast(I32)
+        nc.sync.dma_start(c_pool[:, :C_AHEAD].bitcast(I32), c_dram[:, :C_AHEAD])
         cs_pool = held.tile([P, POOL // 4], I32, name="cs_pool")
         nc.vector.memset(cs_pool[:], 0)
         for r in range(4):
             nc.sync.dma_start(cs_pool[C_PLANE + r : P : QUADRANT, :], c_scales[0, r:16:4, :].bitcast(I32))
-        c_pool = held.tile([P, POOL], U32, name="c_pool")
-        nc.sync.dma_start(c_pool[:].bitcast(I32), c_words[0].rearrange("p n t -> p (n t)").bitcast(I32))
+        nc.sync.dma_start(c_pool[:, C_AHEAD:].bitcast(I32), c_dram[:, C_AHEAD:])
 
         ns_listed = held.tile([P, LISTED], F32, name="ns_listed")
         nc.vector.tensor_copy(ns_listed[:], ns_pool[:].indirect(offsets[:]))

@@ -11,7 +11,6 @@ U16 = mybir.dt.uint16
 U8 = mybir.dt.uint8
 FP8X4 = mybir.dt.float8_e4m3fn_x4
 MULT = mybir.AluOpType.mult
-COPY = mybir.ActivationFunctionType.Copy
 
 P = 128
 PACK = 4
@@ -20,12 +19,13 @@ NQ = 128
 POOL = 2048
 LISTED = 512
 HALF = LISTED // 2
-BLOCKS = LISTED // P
 PER_COLUMN = 16
 QUADRANT = 32
-NS_ROW = P - 1
+RUN = POOL // P
+ROWS = 16
+SCALE_ROWS = P - ROWS
 C_PLANE = 4
-C_AHEAD = 768
+C_AHEAD = 1152
 
 FLOPS = 2 * 2 * D * NQ * LISTED
 
@@ -38,61 +38,57 @@ def tile_attend_neu_bilin_topk_kernel(tc, qT, k_words, k_scales, c_words, c_scal
 
         offsets = held.tile([P, LISTED // PER_COLUMN], U16, name="offsets")
         nc.sync.dma_start(offsets[:], offs)
-        ns_pool = held.tile([P, POOL], F32, name="ns_pool")
-        nc.sync.dma_start(ns_pool[NS_ROW:P, :], ns[0:1, :])
-        q_raw = held.tile([P, PACK, NQ], F32, name="q_raw")
-        nc.sync.dma_start(q_raw[:], qT[0].rearrange("(p j) w -> p j w", j=PACK))
-
         ks_pool = held.tile([P, POOL // 4], I32, name="ks_pool")
-        nc.vector.memset(ks_pool[:], 0)
-        for r in range(4):
-            nc.sync.dma_start(ks_pool[r:P:QUADRANT, :], k_scales[0, r:16:4, :].bitcast(I32))
-
-        identity = held.tile([P, P], F32, name="identity")
-        make_identity(nc, identity[:])
-
+        nc.scalar.dma_start(ks_pool[SCALE_ROWS:P, :], k_scales[0].bitcast(I32))
+        nc.vector.memset(ks_pool[:SCALE_ROWS, :], 0)
+        ns_columns = held.tile([P, RUN], F32, name="ns_columns", tag="in_turn", align_bytes=64)
+        nc.sync.dma_start(ns_columns[:], ns[0].rearrange("(p b) -> p b", b=RUN))
+        cs_pool = held.tile([P, POOL // 4], I32, name="cs_pool")
+        nc.sync.dma_start(cs_pool[SCALE_ROWS:P, :], c_scales[0].bitcast(I32))
         k_pool = held.tile([P, POOL], U32, name="k_pool")
         nc.sync.dma_start(k_pool[:].bitcast(I32), k_words[0].rearrange("p n t -> p (n t)").bitcast(I32))
-        nc.vector.memset(ns_pool[:NS_ROW, :], 0.0)
+        q_raw = held.tile([P, PACK, NQ], F32, name="q_raw")
+        nc.sync.dma_start(q_raw[:], qT[0].rearrange("(p j) w -> p j w", j=PACK))
         c_pool = held.tile([P, POOL], U32, name="c_pool")
         c_dram = c_words[0].rearrange("p n t -> p (n t)").bitcast(I32)
         nc.sync.dma_start(c_pool[:, :C_AHEAD].bitcast(I32), c_dram[:, :C_AHEAD])
-        cs_pool = held.tile([P, POOL // 4], I32, name="cs_pool")
-        nc.vector.memset(cs_pool[:], 0)
-        for r in range(4):
-            nc.sync.dma_start(cs_pool[C_PLANE + r : P : QUADRANT, :], c_scales[0, r:16:4, :].bitcast(I32))
+
+        identity = held.tile([P, P], F32, name="identity")
+        make_identity(nc, identity[:])
+        nc.vector.memset(cs_pool[:SCALE_ROWS, :], 0)
+        planes = held.tile([P, 2 * LISTED // 4], I32, name="planes", align_bytes=64)
+        nc.vector.memset(planes[:], 0)
+        k_plane = planes[:, : LISTED // 4]
+        c_plane = planes[:, LISTED // 4 :]
+
+        def gather_scales(name, pool, plane, first):
+            listed = held.tile([P, LISTED], U8, name=name, align_bytes=64)
+            nc.vector.tensor_copy(listed[:], pool[:].bitcast(U8).indirect(offsets[:]))
+            for g in range(4):
+                nc.sync.dma_start(
+                    plane[QUADRANT * g + first : QUADRANT * g + first + 4, :],
+                    listed[SCALE_ROWS + 4 * g : SCALE_ROWS + 4 * g + 4, :].bitcast(I32),
+                )
+
+        gather_scales("ks_listed", ks_pool, k_plane, 0)
         nc.sync.dma_start(c_pool[:, C_AHEAD:].bitcast(I32), c_dram[:, C_AHEAD:])
 
-        ns_listed = held.tile([P, LISTED], F32, name="ns_listed")
-        nc.vector.tensor_copy(ns_listed[:], ns_pool[:].indirect(offsets[:]))
-        ns_turned = psum.tile([P, BLOCKS, P], F32, name="ns_turned", tag="bank0")
-        for b in range(BLOCKS):
-            nc.tensor.transpose(ns_turned[:, b, :], ns_listed[:, b * P : (b + 1) * P], identity[:])
+        ns_pool = held.tile([P, POOL], F32, name="ns_pool")
+        ns_runs = ns_pool[:].rearrange("q (p b) -> q p b", b=RUN)
+        for j in range(RUN // 4):
+            spread = psum.tile([NQ, 4, P], F32, name=f"spread{j}", tag=f"bank{j}")
+            for i in range(4):
+                column = ns_columns[:, 4 * j + i : 4 * j + i + 1]
+                nc.tensor.transpose(spread[:, i, :], column.to_broadcast([P, P]), identity[:])
+            nc.scalar.copy(ns_runs[:, :, 4 * j : 4 * j + 4], spread[:].rearrange("q i p -> q p i"))
 
-        q_grouped = held.tile([P, NQ, PACK], BF16, name="q_grouped", align_bytes=64)
+        q_grouped = held.tile([P, NQ, PACK], BF16, name="q_grouped", tag="in_turn", align_bytes=64)
         nc.scalar.copy(q_grouped[:], q_raw[:].rearrange("p j w -> p w j"))
-        ns_columns = held.tile([P, BLOCKS], F32, name="ns_columns")
-        nc.scalar.copy(ns_columns[:], ns_turned[:, :, NS_ROW])
-        ns_spread = psum.tile([NQ, 2, P], F32, name="ns_spread")
-        for j in range(2):
-            nc.tensor.transpose(ns_spread[:, j, :], ns_columns[:, 2 + j : 3 + j].to_broadcast([P, P]), identity[:])
-        ns_rows = held.tile([NQ, HALF], F32, name="ns_rows")
-        nc.scalar.copy(ns_rows[:], ns_spread[:].rearrange("q j p -> q (j p)"))
 
-        ks_listed = held.tile([P, LISTED], U8, name="ks_listed", align_bytes=64)
-        nc.vector.tensor_copy(ks_listed[:], ks_pool[:].bitcast(U8).indirect(offsets[:]))
+        gather_scales("cs_listed", cs_pool, c_plane, C_PLANE)
 
-        q_codes = held.tile([P, NQ], U32, name="q_codes", align_bytes=64)
-        q_scales = held.tile([P, NQ], U8, name="q_scales", align_bytes=64)
-        nc.vector.quantize_mx(
-            out=q_codes[:].bitcast(FP8X4), scales=q_scales[:], in_=q_grouped[:].rearrange("p w j -> p (w j)")
-        )
-
-        halves = [slice(h * HALF, (h + 1) * HALF) for h in range(2)]
-        entries = [offsets[:, h * HALF // PER_COLUMN : (h + 1) * HALF // PER_COLUMN] for h in range(2)]
-
-        def by_query_product(name, codes, scales):
-            bank = psum.tile([NQ, HALF], F32, name=name)
+        def product(name, tag, codes, scales):
+            bank = psum.tile([NQ, codes.shape[1]], F32, name=name, tag=tag)
             nc.tensor.matmul_mx(
                 out=bank[:],
                 lhsT=q_codes[:].bitcast(FP8X4),
@@ -104,44 +100,31 @@ def tile_attend_neu_bilin_topk_kernel(tc, qT, k_words, k_scales, c_words, c_scal
             )
             return bank
 
-        k_listed = []
-        for h in range(2):
-            listed = held.tile([P, HALF], U32, name=f"k_listed{h}", align_bytes=64)
-            nc.vector.tensor_copy(listed[:], k_pool[:].indirect(entries[h]))
-            k_listed.append(listed)
+        halves = [slice(h * HALF, (h + 1) * HALF) for h in range(2)]
+        entries = [offsets[:, h * HALF // PER_COLUMN : (h + 1) * HALF // PER_COLUMN] for h in range(2)]
+        k_listed = held.tile([P, LISTED], U32, name="k_listed", align_bytes=64)
+        nc.vector.tensor_copy(k_listed[:], k_pool[:].indirect(offsets[:]))
+        ns_listed = held.tile([NQ, LISTED], F32, name="ns_listed")
+        nc.vector.tensor_copy(ns_listed[:], ns_pool[:].indirect(offsets[:]))
 
-        by_slot = psum.tile([P, 2, NQ], F32, name="by_slot", tag="bank0")
-        for j in range(2):
-            nc.tensor.matmul_mx(
-                out=by_slot[:, j, :],
-                lhsT=k_listed[0][:, j * P : (j + 1) * P].bitcast(FP8X4),
-                lhsT_scale=ks_listed[:, j * P : (j + 1) * P],
-                rhs=q_codes[:].bitcast(FP8X4),
-                rhs_scale=q_scales[:],
-                start=True,
-                stop=True,
-            )
-        gate1 = by_query_product("gate1", k_listed[1][:], ks_listed[:, halves[1]])
-        scaled_by_slot = held.tile([P, 2, NQ], F32, name="scaled_by_slot")
-        by_query = psum.tile([NQ, 2, P], F32, name="by_query")
-        for j in range(2):
-            nc.scalar.activation(scaled_by_slot[:, j, :], by_slot[:, j, :], COPY, scale=ns_columns[:, j : j + 1])
-        for j in range(2):
-            nc.tensor.transpose(by_query[:, j, :], scaled_by_slot[:, j, :], identity[:])
-        scaled0 = held.tile([NQ, HALF], F32, name="scaled0")
-        nc.scalar.copy(scaled0[:], by_query[:].rearrange("q j p -> q (j p)"))
+        q_codes = held.tile([P, NQ], U32, name="q_codes", align_bytes=64)
+        q_scales = held.tile([P, NQ], U8, name="q_scales", align_bytes=64)
+        nc.vector.quantize_mx(
+            out=q_codes[:].bitcast(FP8X4), scales=q_scales[:], in_=q_grouped[:].rearrange("p w j -> p (w j)")
+        )
 
-        cs_listed = held.tile([P, LISTED], U8, name="cs_listed", align_bytes=64)
-        nc.vector.tensor_copy(cs_listed[:], cs_pool[:].bitcast(U8).indirect(offsets[:]))
+        gate = product("gate", "bank2", k_listed[:], k_plane.bitcast(U8))
 
         layer = []
+        c_listed = held.tile([P, LISTED], U32, name="c_listed", tag="in_turn", align_bytes=64)
         for h, cols in enumerate(halves):
-            c_listed = held.tile([P, HALF], U32, name=f"c_listed{h}", tag=f"c_listed{h}", align_bytes=64)
-            nc.vector.tensor_copy(c_listed[:], c_pool[:].indirect(entries[h]))
-            layer.append(by_query_product(f"layer{h}", c_listed[:], cs_listed[C_PLANE:P, cols]))
-        scaled1 = held.tile([NQ, HALF], F32, name="scaled1", tag="c_listed0", align_bytes=64)
-        nc.vector.tensor_tensor(scaled1[:], gate1[:], ns_rows[:], MULT)
-        scaled = [scaled0, scaled1]
+            nc.vector.tensor_copy(c_listed[:, cols], c_pool[:].indirect(entries[h]))
+            layer.append(product(f"layer{h}", f"bank{h}", c_listed[:, cols], c_plane.bitcast(U8)[C_PLANE:P, cols]))
+        scaled = []
+        for h, cols in enumerate(halves):
+            times_ns = held.tile([NQ, HALF], F32, name=f"scaled{h}")
+            nc.vector.tensor_tensor(times_ns[:], gate[:, cols], ns_listed[:, cols], MULT)
+            scaled.append(times_ns)
         for h, cols in enumerate(halves):
             result = held.tile([NQ, HALF], F32, name=f"result{h}")
             nc.vector.tensor_tensor(result[:], layer[h][:], scaled[h][:], MULT)

@@ -25,7 +25,7 @@ RUN = POOL // P
 ROWS = 16
 SCALE_ROWS = P - ROWS
 C_PLANE = 4
-C_AHEAD = 1152
+C_AHEAD = 1024
 
 FLOPS = 2 * 2 * D * NQ * LISTED
 
@@ -39,15 +39,15 @@ def tile_attend_neu_bilin_topk_kernel(tc, qT, k_words, k_scales, c_words, c_scal
         offsets = held.tile([P, LISTED // PER_COLUMN], U16, name="offsets")
         nc.sync.dma_start(offsets[:], offs)
         ks_pool = held.tile([P, POOL // 4], I32, name="ks_pool")
-        nc.scalar.dma_start(ks_pool[SCALE_ROWS:P, :], k_scales[0].bitcast(I32))
+        nc.sync.dma_start(ks_pool[SCALE_ROWS:P, :], k_scales[0].bitcast(I32))
         nc.vector.memset(ks_pool[:SCALE_ROWS, :], 0)
         ns_columns = held.tile([P, RUN], F32, name="ns_columns", tag="in_turn", align_bytes=64)
-        nc.sync.dma_start(ns_columns[:], ns[0].rearrange("(p b) -> p b", b=RUN))
+        nc.scalar.dma_start(ns_columns[:], ns[0].rearrange("(p b) -> p b", b=RUN))
         cs_pool = held.tile([P, POOL // 4], I32, name="cs_pool")
-        nc.sync.dma_start(cs_pool[SCALE_ROWS:P, :], c_scales[0].bitcast(I32))
+        nc.scalar.dma_start(cs_pool[SCALE_ROWS:P, :], c_scales[0].bitcast(I32))
         k_pool = held.tile([P, POOL], U32, name="k_pool")
         nc.sync.dma_start(k_pool[:].bitcast(I32), k_words[0].rearrange("p n t -> p (n t)").bitcast(I32))
-        q_raw = held.tile([P, PACK, NQ], F32, name="q_raw")
+        q_raw = held.tile([P, PACK, NQ], F32, name="q_raw", tag="q_raw", align_bytes=64)
         nc.sync.dma_start(q_raw[:], qT[0].rearrange("(p j) w -> p j w", j=PACK))
         c_pool = held.tile([P, POOL], U32, name="c_pool")
         c_dram = c_words[0].rearrange("p n t -> p (n t)").bitcast(I32)
@@ -116,7 +116,7 @@ def tile_attend_neu_bilin_topk_kernel(tc, qT, k_words, k_scales, c_words, c_scal
         gate = product("gate", "bank2", k_listed[:], k_plane.bitcast(U8))
 
         layer = []
-        c_listed = held.tile([P, LISTED], U32, name="c_listed", tag="in_turn", align_bytes=64)
+        c_listed = held.tile([P, LISTED], U32, name="c_listed", tag="q_raw", align_bytes=64)
         for h, cols in enumerate(halves):
             nc.vector.tensor_copy(c_listed[:, cols], c_pool[:].indirect(entries[h]))
             layer.append(product(f"layer{h}", f"bank{h}", c_listed[:, cols], c_plane.bitcast(U8)[C_PLANE:P, cols]))

@@ -23,7 +23,8 @@ PER_COLUMN = 16
 QUADRANT = 32
 RUN = POOL // P
 ROWS = 16
-SCALE_ROWS = P - ROWS
+K_ROWS = P - ROWS
+C_ROWS = P // 2 - ROWS
 C_PLANE = 4
 C_AHEAD = 1024
 
@@ -39,12 +40,12 @@ def tile_attend_neu_bilin_topk_kernel(tc, qT, k_words, k_scales, c_words, c_scal
         offsets = held.tile([P, LISTED // PER_COLUMN], U16, name="offsets")
         nc.sync.dma_start(offsets[:], offs)
         ks_pool = held.tile([P, POOL // 4], I32, name="ks_pool")
-        nc.sync.dma_start(ks_pool[SCALE_ROWS:P, :], k_scales[0].bitcast(I32))
-        nc.vector.memset(ks_pool[:SCALE_ROWS, :], 0)
+        nc.sync.dma_start(ks_pool[K_ROWS:P, :], k_scales[0].bitcast(I32))
+        nc.vector.memset(ks_pool[:K_ROWS, :], 0)
         ns_columns = held.tile([P, RUN], F32, name="ns_columns", tag="in_turn", align_bytes=64)
         nc.scalar.dma_start(ns_columns[:], ns[0].rearrange("(p b) -> p b", b=RUN))
         cs_pool = held.tile([P, POOL // 4], I32, name="cs_pool")
-        nc.scalar.dma_start(cs_pool[SCALE_ROWS:P, :], c_scales[0].bitcast(I32))
+        nc.scalar.dma_start(cs_pool[C_ROWS : P // 2, :], c_scales[0].bitcast(I32))
         k_pool = held.tile([P, POOL], U32, name="k_pool")
         nc.sync.dma_start(k_pool[:].bitcast(I32), k_words[0].rearrange("p n t -> p (n t)").bitcast(I32))
         q_raw = held.tile([P, PACK, NQ], F32, name="q_raw", tag="q_raw", align_bytes=64)
@@ -55,22 +56,23 @@ def tile_attend_neu_bilin_topk_kernel(tc, qT, k_words, k_scales, c_words, c_scal
 
         identity = held.tile([P, P], F32, name="identity")
         make_identity(nc, identity[:])
-        nc.vector.memset(cs_pool[:SCALE_ROWS, :], 0)
+        nc.vector.memset(cs_pool[:C_ROWS, :], 0)
+        nc.vector.memset(cs_pool[P // 2 :, :], 0)
         planes = held.tile([P, 2 * LISTED // 4], I32, name="planes", align_bytes=64)
         nc.vector.memset(planes[:], 0)
         k_plane = planes[:, : LISTED // 4]
         c_plane = planes[:, LISTED // 4 :]
 
-        def gather_scales(name, pool, plane, first):
+        def gather_scales(name, pool, rows, plane, first):
             listed = held.tile([P, LISTED], U8, name=name, align_bytes=64)
             nc.vector.tensor_copy(listed[:], pool[:].bitcast(U8).indirect(offsets[:]))
             for g in range(4):
                 nc.sync.dma_start(
                     plane[QUADRANT * g + first : QUADRANT * g + first + 4, :],
-                    listed[SCALE_ROWS + 4 * g : SCALE_ROWS + 4 * g + 4, :].bitcast(I32),
+                    listed[rows + 4 * g : rows + 4 * g + 4, :].bitcast(I32),
                 )
 
-        gather_scales("ks_listed", ks_pool, k_plane, 0)
+        gather_scales("ks_listed", ks_pool, K_ROWS, k_plane, 0)
         nc.sync.dma_start(c_pool[:, C_AHEAD:].bitcast(I32), c_dram[:, C_AHEAD:])
 
         ns_pool = held.tile([P, POOL], F32, name="ns_pool")
@@ -85,7 +87,7 @@ def tile_attend_neu_bilin_topk_kernel(tc, qT, k_words, k_scales, c_words, c_scal
         q_grouped = held.tile([P, NQ, PACK], BF16, name="q_grouped", tag="in_turn", align_bytes=64)
         nc.scalar.copy(q_grouped[:], q_raw[:].rearrange("p j w -> p w j"))
 
-        gather_scales("cs_listed", cs_pool, c_plane, C_PLANE)
+        gather_scales("cs_listed", cs_pool, C_ROWS, c_plane, C_PLANE)
 
         def product(name, tag, codes, scales):
             bank = psum.tile([NQ, codes.shape[1]], F32, name=name, tag=tag)

@@ -19,6 +19,7 @@ NQ = 128
 POOL = 2048
 LISTED = 512
 HALF = LISTED // 2
+BODY = LISTED - LISTED // 4
 PER_COLUMN = 16
 QUADRANT = 32
 RUN = POOL // P
@@ -106,8 +107,8 @@ def tile_attend_neu_bilin_topk_kernel(tc, qT, k_words, k_scales, c_words, c_scal
         entries = [offsets[:, h * HALF // PER_COLUMN : (h + 1) * HALF // PER_COLUMN] for h in range(2)]
         k_listed = held.tile([P, LISTED], U32, name="k_listed", align_bytes=64)
         nc.vector.tensor_copy(k_listed[:], k_pool[:].indirect(offsets[:]))
-        ns_listed = held.tile([NQ, LISTED], F32, name="ns_listed")
-        nc.vector.tensor_copy(ns_listed[:], ns_pool[:].indirect(offsets[:]))
+        ns_listed = held.tile([NQ, BODY], F32, name="ns_listed")
+        nc.vector.tensor_copy(ns_listed[:], ns_pool[:].indirect(offsets[:, : BODY // PER_COLUMN]))
 
         q_codes = held.tile([P, NQ], U32, name="q_codes", align_bytes=64)
         q_scales = held.tile([P, NQ], U8, name="q_scales", align_bytes=64)
@@ -115,18 +116,32 @@ def tile_attend_neu_bilin_topk_kernel(tc, qT, k_words, k_scales, c_words, c_scal
             out=q_codes[:].bitcast(FP8X4), scales=q_scales[:], in_=q_grouped[:].rearrange("p w j -> p (w j)")
         )
 
-        gate = product("gate", "bank2", k_listed[:], k_plane.bitcast(U8))
+        gate_last = product("gate_last", "bank3", k_listed[:, BODY:], k_plane.bitcast(U8)[:, BODY:])
+        gate_copy = held.tile([NQ, LISTED - BODY], F32, name="gate_copy")
+        nc.scalar.copy(gate_copy[:], gate_last[:])
+        gate = psum.tile([NQ, BODY], F32, name="gate", tag="bank2")
+        for cols in (slice(0, HALF), slice(HALF, BODY)):
+            nc.tensor.matmul_mx(
+                out=gate[:, cols],
+                lhsT=q_codes[:].bitcast(FP8X4),
+                lhsT_scale=q_scales[:],
+                rhs=k_listed[:, cols].bitcast(FP8X4),
+                rhs_scale=k_plane.bitcast(U8)[:, cols],
+                start=True,
+                stop=True,
+            )
 
         layer = []
         c_listed = held.tile([P, LISTED], U32, name="c_listed", tag="q_raw", align_bytes=64)
         for h, cols in enumerate(halves):
             nc.vector.tensor_copy(c_listed[:, cols], c_pool[:].indirect(entries[h]))
             layer.append(product(f"layer{h}", f"bank{h}", c_listed[:, cols], c_plane.bitcast(U8)[C_PLANE:P, cols]))
-        scaled = []
-        for h, cols in enumerate(halves):
-            times_ns = held.tile([NQ, HALF], F32, name=f"scaled{h}")
-            nc.vector.tensor_tensor(times_ns[:], gate[:, cols], ns_listed[:, cols], MULT)
-            scaled.append(times_ns)
+        scaled = [held.tile([NQ, HALF], F32, name=f"scaled{h}") for h in range(2)]
+        nc.vector.tensor_tensor(scaled[0][:], gate[:, :HALF], ns_listed[:, :HALF], MULT)
+        nc.vector.tensor_tensor(scaled[1][:, : BODY - HALF], gate[:, HALF:], ns_listed[:, HALF:], MULT)
+        nc.vector.tensor_tensor(
+            scaled[1][:, BODY - HALF :], ns_pool[:].indirect(offsets[:, BODY // PER_COLUMN :]), gate_copy[:], MULT
+        )
         for h, cols in enumerate(halves):
             result = held.tile([NQ, HALF], F32, name=f"result{h}")
             nc.vector.tensor_tensor(result[:], layer[h][:], scaled[h][:], MULT)

@@ -41,16 +41,16 @@ def tile_attend_neu_bilin_topk_kernel(tc, qT, k_words, k_scales, c_words, c_scal
         offsets = held.tile([P, LISTED // PER_COLUMN], U16, name="offsets")
         nc.sync.dma_start(offsets[:], offs)
         ks_pool = held.tile([P, POOL // 4], I32, name="ks_pool")
-        nc.sync.dma_start(ks_pool[K_ROWS:P, :], k_scales[0].bitcast(I32))
+        nc.scalar.dma_start(ks_pool[K_ROWS:P, :], k_scales[0].bitcast(I32))
         nc.vector.memset(ks_pool[:K_ROWS, :], 0)
         ns_columns = held.tile([P, RUN], F32, name="ns_columns", tag="in_turn", align_bytes=64)
-        nc.scalar.dma_start(ns_columns[:], ns[0].rearrange("(p b) -> p b", b=RUN))
+        nc.sync.dma_start(ns_columns[:], ns[0].rearrange("(p b) -> p b", b=RUN))
         cs_pool = held.tile([P, POOL // 4], I32, name="cs_pool")
-        nc.scalar.dma_start(cs_pool[C_ROWS : P // 2, :], c_scales[0].bitcast(I32))
+        nc.sync.dma_start(cs_pool[C_ROWS : P // 2, :], c_scales[0].bitcast(I32))
         k_pool = held.tile([P, POOL], U32, name="k_pool")
         nc.sync.dma_start(k_pool[:].bitcast(I32), k_words[0].rearrange("p n t -> p (n t)").bitcast(I32))
         q_raw = held.tile([P, PACK, NQ], F32, name="q_raw", tag="q_raw", align_bytes=64)
-        nc.sync.dma_start(q_raw[:], qT[0].rearrange("(p j) w -> p j w", j=PACK))
+        nc.scalar.dma_start(q_raw[:], qT[0].rearrange("(p j) w -> p j w", j=PACK))
         c_pool = held.tile([P, POOL], U32, name="c_pool")
         c_dram = c_words[0].rearrange("p n t -> p (n t)").bitcast(I32)
         nc.sync.dma_start(c_pool[:, :C_AHEAD].bitcast(I32), c_dram[:, :C_AHEAD])

@@ -11,6 +11,7 @@ U16 = mybir.dt.uint16
 U8 = mybir.dt.uint8
 FP8X4 = mybir.dt.float8_e4m3fn_x4
 MULT = mybir.AluOpType.mult
+COPY = mybir.ActivationFunctionType.Copy
 
 P = 128
 PACK = 4
@@ -19,15 +20,17 @@ NQ = 128
 POOL = 2048
 LISTED = 512
 HALF = LISTED // 2
-BODY = LISTED - LISTED // 4
 PER_COLUMN = 16
 QUADRANT = 32
-RUN = POOL // P
 ROWS = 16
 K_ROWS = P - ROWS
 C_ROWS = P // 2 - ROWS
 C_PLANE = 4
 C_AHEAD = 1024
+NS_ROW = P - 1
+ODD = POOL // 8 - 1
+BLOCKS = LISTED // P
+PIECES = (slice(0, 256), slice(256, 384), slice(384, 512))
 
 FLOPS = 2 * 2 * D * NQ * LISTED
 
@@ -42,73 +45,52 @@ def tile_attend_neu_bilin_topk_kernel(tc, qT, k_words, k_scales, c_words, c_scal
         nc.sync.dma_start(offsets[:], offs)
         ks_pool = held.tile([P, POOL // 4], I32, name="ks_pool")
         nc.scalar.dma_start(ks_pool[K_ROWS:P, :], k_scales[0].bitcast(I32))
-        nc.vector.memset(ks_pool[:K_ROWS, :], 0)
-        ns_columns = held.tile([P, RUN], F32, name="ns_columns", tag="in_turn", align_bytes=64)
-        nc.sync.dma_start(ns_columns[:], ns[0].rearrange("(p b) -> p b", b=RUN))
+        ns_pool = held.tile([P, POOL], F32, name="ns_pool")
+        nc.sync.dma_start(ns_pool[NS_ROW:P, :], ns[0:1, :])
         cs_pool = held.tile([P, POOL // 4], I32, name="cs_pool")
         nc.sync.dma_start(cs_pool[C_ROWS : P // 2, :], c_scales[0].bitcast(I32))
+        q_raw = held.tile([P, PACK, NQ], F32, name="q_raw")
+        nc.scalar.dma_start(q_raw[:], qT[0].rearrange("(p j) w -> p j w", j=PACK))
         k_pool = held.tile([P, POOL], U32, name="k_pool")
         nc.sync.dma_start(k_pool[:].bitcast(I32), k_words[0].rearrange("p n t -> p (n t)").bitcast(I32))
-        q_raw = held.tile([P, PACK, NQ], F32, name="q_raw", tag="q_raw", align_bytes=64)
-        nc.scalar.dma_start(q_raw[:], qT[0].rearrange("(p j) w -> p j w", j=PACK))
         c_pool = held.tile([P, POOL], U32, name="c_pool")
         c_dram = c_words[0].rearrange("p n t -> p (n t)").bitcast(I32)
         nc.sync.dma_start(c_pool[:, :C_AHEAD].bitcast(I32), c_dram[:, :C_AHEAD])
 
         identity = held.tile([P, P], F32, name="identity")
         make_identity(nc, identity[:])
-        nc.vector.memset(cs_pool[:C_ROWS, :], 0)
-        nc.vector.memset(cs_pool[P // 2 :, :], 0)
+        for unused in (ks_pool[:K_ROWS, :], cs_pool[:C_ROWS, :], cs_pool[P // 2 :, :]):
+            nc.vector.memset(unused[:, :ODD], 0)
+            nc.vector.memset(unused[:, ODD:], 0)
         planes = held.tile([P, 2 * LISTED // 4], I32, name="planes", align_bytes=64)
-        nc.vector.memset(planes[:], 0)
+        nc.gpsimd.memset(planes[:], 0)
+        nc.gpsimd.memset(ns_pool[:NS_ROW, :], 0.0)
         k_plane = planes[:, : LISTED // 4]
         c_plane = planes[:, LISTED // 4 :]
 
-        def gather_scales(name, pool, rows, plane, first):
+        def gather_scales(name, pool, rows, plane, first, queues):
             listed = held.tile([P, LISTED], U8, name=name, align_bytes=64)
             nc.vector.tensor_copy(listed[:], pool[:].bitcast(U8).indirect(offsets[:]))
-            for g in range(4):
-                nc.sync.dma_start(
+            for g, queue in enumerate(queues):
+                queue.dma_start(
                     plane[QUADRANT * g + first : QUADRANT * g + first + 4, :],
                     listed[rows + 4 * g : rows + 4 * g + 4, :].bitcast(I32),
                 )
 
-        gather_scales("ks_listed", ks_pool, K_ROWS, k_plane, 0)
+        gather_scales("ks_listed", ks_pool, K_ROWS, k_plane, 0, (nc.sync,) * 4)
         nc.sync.dma_start(c_pool[:, C_AHEAD:].bitcast(I32), c_dram[:, C_AHEAD:])
+        gather_scales("cs_listed", cs_pool, C_ROWS, c_plane, C_PLANE, (nc.sync,) * 4)
 
-        ns_pool = held.tile([P, POOL], F32, name="ns_pool")
-        ns_runs = ns_pool[:].rearrange("q (p b) -> q p b", b=RUN)
-        for j in range(RUN // 4):
-            spread = psum.tile([NQ, 4, P], F32, name=f"spread{j}", tag=f"bank{j}")
-            for i in range(4):
-                column = ns_columns[:, 4 * j + i : 4 * j + i + 1]
-                nc.tensor.transpose(spread[:, i, :], column.to_broadcast([P, P]), identity[:])
-            nc.scalar.copy(ns_runs[:, :, 4 * j : 4 * j + 4], spread[:].rearrange("q i p -> q p i"))
-
-        q_grouped = held.tile([P, NQ, PACK], BF16, name="q_grouped", tag="in_turn", align_bytes=64)
+        q_grouped = held.tile([P, NQ, PACK], BF16, name="q_grouped", align_bytes=64)
         nc.scalar.copy(q_grouped[:], q_raw[:].rearrange("p j w -> p w j"))
+        ns_listed = held.tile([P, LISTED], F32, name="ns_listed")
+        nc.scalar.activation(ns_listed[:], ns_pool[:].indirect(offsets[:]), COPY)
 
-        gather_scales("cs_listed", cs_pool, C_ROWS, c_plane, C_PLANE)
-
-        def product(name, tag, codes, scales):
-            bank = psum.tile([NQ, codes.shape[1]], F32, name=name, tag=tag)
-            nc.tensor.matmul_mx(
-                out=bank[:],
-                lhsT=q_codes[:].bitcast(FP8X4),
-                lhsT_scale=q_scales[:],
-                rhs=codes.bitcast(FP8X4),
-                rhs_scale=scales,
-                start=True,
-                stop=True,
-            )
-            return bank
-
-        halves = [slice(h * HALF, (h + 1) * HALF) for h in range(2)]
-        entries = [offsets[:, h * HALF // PER_COLUMN : (h + 1) * HALF // PER_COLUMN] for h in range(2)]
-        k_listed = held.tile([P, LISTED], U32, name="k_listed", align_bytes=64)
-        nc.vector.tensor_copy(k_listed[:], k_pool[:].indirect(offsets[:]))
-        ns_listed = held.tile([NQ, BODY], F32, name="ns_listed")
-        nc.vector.tensor_copy(ns_listed[:], ns_pool[:].indirect(offsets[:, : BODY // PER_COLUMN]))
+        ns_columns = held.tile([P, BLOCKS], F32, name="ns_columns")
+        for b in range(BLOCKS):
+            turned = psum.tile([P, P], F32, name=f"turned{b}", tag=f"bank{b}")
+            nc.tensor.transpose(turned[:], ns_listed[:, b * P : (b + 1) * P], identity[:])
+            nc.scalar.copy(ns_columns[:, b : b + 1], turned[:, NS_ROW:P])
 
         q_codes = held.tile([P, NQ], U32, name="q_codes", align_bytes=64)
         q_scales = held.tile([P, NQ], U8, name="q_scales", align_bytes=64)
@@ -116,34 +98,52 @@ def tile_attend_neu_bilin_topk_kernel(tc, qT, k_words, k_scales, c_words, c_scal
             out=q_codes[:].bitcast(FP8X4), scales=q_scales[:], in_=q_grouped[:].rearrange("p w j -> p (w j)")
         )
 
-        gate_last = product("gate_last", "bank3", k_listed[:, BODY:], k_plane.bitcast(U8)[:, BODY:])
-        gate_copy = held.tile([NQ, LISTED - BODY], F32, name="gate_copy")
-        nc.scalar.copy(gate_copy[:], gate_last[:])
-        gate = psum.tile([NQ, BODY], F32, name="gate", tag="bank2")
-        for cols in (slice(0, HALF), slice(HALF, BODY)):
+        def listed_offsets(cols):
+            return offsets[:, cols.start // PER_COLUMN : cols.stop // PER_COLUMN]
+
+        k_listed = held.tile([P, LISTED], U32, name="k_listed", align_bytes=64)
+        gate = []
+        for b in range(BLOCKS):
+            if b % 2 == 0:
+                half = slice(b * P, b * P + HALF)
+                nc.vector.tensor_copy(k_listed[:, half], k_pool[:].indirect(listed_offsets(half)))
+            cols = slice(b * P, (b + 1) * P)
+            gate.append(psum.tile([P, NQ], F32, name=f"gate{b}", tag=f"bank{b}"))
             nc.tensor.matmul_mx(
-                out=gate[:, cols],
-                lhsT=q_codes[:].bitcast(FP8X4),
-                lhsT_scale=q_scales[:],
-                rhs=k_listed[:, cols].bitcast(FP8X4),
-                rhs_scale=k_plane.bitcast(U8)[:, cols],
+                out=gate[b][:],
+                lhsT=k_listed[:, cols].bitcast(FP8X4),
+                lhsT_scale=k_plane.bitcast(U8)[:, cols],
+                rhs=q_codes[:].bitcast(FP8X4),
+                rhs_scale=q_scales[:],
                 start=True,
                 stop=True,
             )
+        by_slot = held.tile([P, BLOCKS, NQ], F32, name="by_slot")
+        for b in range(BLOCKS):
+            nc.scalar.activation(by_slot[:, b, :], gate[b][:], COPY, scale=ns_columns[:, b : b + 1])
+        scaled = held.tile([NQ, LISTED], F32, name="scaled")
+        for n, cols in enumerate(PIECES):
+            back = psum.tile([NQ, cols.stop - cols.start], F32, name=f"back{n}", tag=f"bank{(4, 5, 0)[n]}")
+            for b in range(cols.start // P, cols.stop // P):
+                nc.tensor.transpose(back[:, b * P - cols.start : (b + 1) * P - cols.start], by_slot[:, b, :], identity[:])
+            nc.scalar.copy(scaled[:, cols], back[:])
 
+        c_listed = held.tile([P, LISTED], U32, name="c_listed", align_bytes=64)
         layer = []
-        c_listed = held.tile([P, LISTED], U32, name="c_listed", tag="q_raw", align_bytes=64)
-        for h, cols in enumerate(halves):
-            nc.vector.tensor_copy(c_listed[:, cols], c_pool[:].indirect(entries[h]))
-            layer.append(product(f"layer{h}", f"bank{h}", c_listed[:, cols], c_plane.bitcast(U8)[C_PLANE:P, cols]))
-        scaled = [held.tile([NQ, HALF], F32, name=f"scaled{h}") for h in range(2)]
-        nc.vector.tensor_tensor(scaled[0][:], gate[:, :HALF], ns_listed[:, :HALF], MULT)
-        nc.vector.tensor_tensor(scaled[1][:, : BODY - HALF], gate[:, HALF:], ns_listed[:, HALF:], MULT)
-        nc.vector.tensor_tensor(
-            scaled[1][:, BODY - HALF :], ns_pool[:].indirect(offsets[:, BODY // PER_COLUMN :]), gate_copy[:], MULT
-        )
-        for h, cols in enumerate(halves):
-            result = held.tile([NQ, HALF], F32, name=f"result{h}")
-            nc.vector.tensor_tensor(result[:], layer[h][:], scaled[h][:], MULT)
-            queue = nc.sync if h == 0 else nc.scalar
-            queue.dma_start(out[0, :, cols], result[:])
+        for n, cols in enumerate(PIECES):
+            nc.vector.tensor_copy(c_listed[:, cols], c_pool[:].indirect(listed_offsets(cols)))
+            layer.append(psum.tile([NQ, cols.stop - cols.start], F32, name=f"layer{n}", tag=f"bank{(6, 7, 1)[n]}"))
+            nc.tensor.matmul_mx(
+                out=layer[n][:],
+                lhsT=q_codes[:].bitcast(FP8X4),
+                lhsT_scale=q_scales[:],
+                rhs=c_listed[:, cols].bitcast(FP8X4),
+                rhs_scale=c_plane.bitcast(U8)[C_PLANE:P, cols],
+                start=True,
+                stop=True,
+            )
+        result = held.tile([NQ, LISTED], F32, name="result")
+        for n, cols in enumerate(PIECES):
+            nc.vector.tensor_tensor(result[:, cols], layer[n][:], scaled[:, cols], MULT)
+            queue = nc.scalar if n == 1 else nc.sync
+            queue.dma_start(out[0, :, cols], result[:, cols])

@@ -39,15 +39,16 @@ def tile_attend_neu_bilin_topk_kernel(tc, qT, k_words, k_scales, c_words, c_scal
     nc = tc.nc
     with ExitStack() as ctx:
         held = ctx.enter_context(tc.tile_pool(name="held", bufs=1))
+        in_turn = ctx.enter_context(tc.tile_pool(name="in_turn", bufs=1))
         psum = ctx.enter_context(tc.psum_pool(name="psum", bufs=1))
 
+        ns_pool = held.tile([P, POOL], F32, name="ns_pool")
+        nc.sync.dma_start(ns_pool[NS_ROW:P, :], ns[0:1, :])
         offsets = held.tile([P, LISTED // PER_COLUMN], U16, name="offsets")
         nc.sync.dma_start(offsets[:], offs)
         ks_pool = held.tile([P, POOL // 4], I32, name="ks_pool")
         nc.scalar.dma_start(ks_pool[K_ROWS:P, :], k_scales[0].bitcast(I32))
-        ns_pool = held.tile([P, POOL], F32, name="ns_pool")
-        nc.sync.dma_start(ns_pool[NS_ROW:P, :], ns[0:1, :])
-        cs_pool = held.tile([P, POOL // 4], I32, name="cs_pool")
+        cs_pool = in_turn.tile([P, POOL // 4], I32, name="cs_pool", align_bytes=64, offset=0)
         nc.sync.dma_start(cs_pool[C_ROWS : P // 2, :], c_scales[0].bitcast(I32))
         q_raw = held.tile([P, PACK, NQ], F32, name="q_raw")
         nc.scalar.dma_start(q_raw[:], qT[0].rearrange("(p j) w -> p j w", j=PACK))
@@ -57,16 +58,20 @@ def tile_attend_neu_bilin_topk_kernel(tc, qT, k_words, k_scales, c_words, c_scal
         c_dram = c_words[0].rearrange("p n t -> p (n t)").bitcast(I32)
         nc.sync.dma_start(c_pool[:, :C_AHEAD].bitcast(I32), c_dram[:, :C_AHEAD])
 
-        identity = held.tile([P, P], F32, name="identity")
-        make_identity(nc, identity[:])
-        for unused in (ks_pool[:K_ROWS, :], cs_pool[:C_ROWS, :], cs_pool[P // 2 :, :]):
+        for unused in (ks_pool[:K_ROWS, :], cs_pool[P // 2 :, :]):
             nc.vector.memset(unused[:, :ODD], 0)
             nc.vector.memset(unused[:, ODD:], 0)
         planes = held.tile([P, 2 * LISTED // 4], I32, name="planes", align_bytes=64)
         nc.gpsimd.memset(planes[:], 0)
+        nc.gpsimd.memset(cs_pool[:C_ROWS, :], 0)
         nc.gpsimd.memset(ns_pool[:NS_ROW, :], 0.0)
+        identity = held.tile([P, P], F32, name="identity")
+        make_identity(nc, identity[:])
         k_plane = planes[:, : LISTED // 4]
         c_plane = planes[:, LISTED // 4 :]
+
+        def listed_offsets(cols):
+            return offsets[:, cols.start // PER_COLUMN : cols.stop // PER_COLUMN]
 
         def gather_scales(name, pool, rows, plane, first, queues):
             listed = held.tile([P, LISTED], U8, name=name, align_bytes=64)
@@ -84,7 +89,9 @@ def tile_attend_neu_bilin_topk_kernel(tc, qT, k_words, k_scales, c_words, c_scal
         q_grouped = held.tile([P, NQ, PACK], BF16, name="q_grouped", align_bytes=64)
         nc.scalar.copy(q_grouped[:], q_raw[:].rearrange("p j w -> p w j"))
         ns_listed = held.tile([P, LISTED], F32, name="ns_listed")
-        nc.scalar.activation(ns_listed[:], ns_pool[:].indirect(offsets[:]), COPY)
+        for h in range(2):
+            half = slice(h * HALF, (h + 1) * HALF)
+            nc.scalar.activation(ns_listed[:, half], ns_pool[:].indirect(listed_offsets(half)), COPY)
 
         ns_columns = held.tile([P, BLOCKS], F32, name="ns_columns")
         for b in range(BLOCKS):
@@ -92,16 +99,13 @@ def tile_attend_neu_bilin_topk_kernel(tc, qT, k_words, k_scales, c_words, c_scal
             nc.tensor.transpose(turned[:], ns_listed[:, b * P : (b + 1) * P], identity[:])
             nc.scalar.copy(ns_columns[:, b : b + 1], turned[:, NS_ROW:P])
 
-        q_codes = held.tile([P, NQ], U32, name="q_codes", align_bytes=64)
+        q_codes = in_turn.tile([P, NQ], U32, name="q_codes", align_bytes=64, offset=0)
         q_scales = held.tile([P, NQ], U8, name="q_scales", align_bytes=64)
         nc.vector.quantize_mx(
             out=q_codes[:].bitcast(FP8X4), scales=q_scales[:], in_=q_grouped[:].rearrange("p w j -> p (w j)")
         )
 
-        def listed_offsets(cols):
-            return offsets[:, cols.start // PER_COLUMN : cols.stop // PER_COLUMN]
-
-        k_listed = held.tile([P, LISTED], U32, name="k_listed", align_bytes=64)
+        k_listed = in_turn.tile([P, LISTED], U32, name="k_listed", align_bytes=64, offset=POOL // 2)
         gate = []
         for b in range(BLOCKS):
             if b % 2 == 0:

@@ -23,8 +23,8 @@ HALF = LISTED // 2
 PER_COLUMN = 16
 QUADRANT = 32
 ROWS = 16
-K_ROWS = P - ROWS
-C_ROWS = P // 2 - ROWS
+K_ROWS = P // 2 - ROWS
+C_ROWS = P - ROWS
 C_PLANE = 4
 C_AHEAD = 1024
 NS_ROW = P - 1
@@ -47,9 +47,9 @@ def tile_attend_neu_bilin_topk_kernel(tc, qT, k_words, k_scales, c_words, c_scal
         offsets = held.tile([P, LISTED // PER_COLUMN], U16, name="offsets")
         nc.sync.dma_start(offsets[:], offs)
         ks_pool = held.tile([P, POOL // 4], I32, name="ks_pool")
-        nc.scalar.dma_start(ks_pool[K_ROWS:P, :], k_scales[0].bitcast(I32))
+        nc.scalar.dma_start(ks_pool[K_ROWS : P // 2, :], k_scales[0].bitcast(I32))
         cs_pool = in_turn.tile([P, POOL // 4], I32, name="cs_pool", align_bytes=64, offset=0)
-        nc.sync.dma_start(cs_pool[C_ROWS : P // 2, :], c_scales[0].bitcast(I32))
+        nc.sync.dma_start(cs_pool[C_ROWS:P, :], c_scales[0].bitcast(I32))
         q_raw = held.tile([P, PACK, NQ], F32, name="q_raw")
         nc.scalar.dma_start(q_raw[:], qT[0].rearrange("(p j) w -> p j w", j=PACK))
         k_pool = held.tile([P, POOL], U32, name="k_pool")
@@ -58,7 +58,7 @@ def tile_attend_neu_bilin_topk_kernel(tc, qT, k_words, k_scales, c_words, c_scal
         c_dram = c_words[0].rearrange("p n t -> p (n t)").bitcast(I32)
         nc.sync.dma_start(c_pool[:, :C_AHEAD].bitcast(I32), c_dram[:, :C_AHEAD])
 
-        for unused in (ks_pool[:K_ROWS, :], cs_pool[P // 2 :, :]):
+        for unused in (ks_pool[:K_ROWS, :], ks_pool[P // 2 :, :]):
             nc.vector.memset(unused[:, :ODD], 0)
             nc.vector.memset(unused[:, ODD:], 0)
         planes = held.tile([P, 2 * LISTED // 4], I32, name="planes", align_bytes=64)

from contextlib import ExitStack

import concourse.mybir as mybir
from concourse.masks import make_identity

F32 = mybir.dt.float32
BF16 = mybir.dt.bfloat16
I32 = mybir.dt.int32
U32 = mybir.dt.uint32
U16 = mybir.dt.uint16
U8 = mybir.dt.uint8
FP8X4 = mybir.dt.float8_e4m3fn_x4
MULT = mybir.AluOpType.mult
COPY = mybir.ActivationFunctionType.Copy

P = 128
PACK = 4
D = P * PACK
NQ = 128
POOL = 2048
LISTED = 512
HALF = LISTED // 2
PER_COLUMN = 16
QUADRANT = 32
ROWS = 16
K_ROWS = P // 2 - ROWS
C_ROWS = P - ROWS
C_PLANE = 4
C_AHEAD = 1024
NS_ROW = P - 1
ODD = POOL // 8 - 1
BLOCKS = LISTED // P
PIECES = (slice(0, 256), slice(256, 384), slice(384, 512))

FLOPS = 2 * 2 * D * NQ * LISTED


def tile_attend_neu_bilin_topk_kernel(tc, qT, k_words, k_scales, c_words, c_scales, ns, offs, out):
    nc = tc.nc
    with ExitStack() as ctx:
        held = ctx.enter_context(tc.tile_pool(name="held", bufs=1))
        in_turn = ctx.enter_context(tc.tile_pool(name="in_turn", bufs=1))
        psum = ctx.enter_context(tc.psum_pool(name="psum", bufs=1))

        ns_pool = held.tile([P, POOL], F32, name="ns_pool")
        nc.sync.dma_start(ns_pool[NS_ROW:P, :], ns[0:1, :])
        offsets = held.tile([P, LISTED // PER_COLUMN], U16, name="offsets")
        nc.sync.dma_start(offsets[:], offs)
        ks_pool = held.tile([P, POOL // 4], I32, name="ks_pool")
        nc.scalar.dma_start(ks_pool[K_ROWS : P // 2, :], k_scales[0].bitcast(I32))
        cs_pool = in_turn.tile([P, POOL // 4], I32, name="cs_pool", align_bytes=64, offset=0)
        nc.sync.dma_start(cs_pool[C_ROWS:P, :], c_scales[0].bitcast(I32))
        q_raw = held.tile([P, PACK, NQ], F32, name="q_raw")
        nc.scalar.dma_start(q_raw[:], qT[0].rearrange("(p j) w -> p j w", j=PACK))
        k_pool = held.tile([P, POOL], U32, name="k_pool")
        nc.sync.dma_start(k_pool[:].bitcast(I32), k_words[0].rearrange("p n t -> p (n t)").bitcast(I32))
        c_pool = held.tile([P, POOL], U32, name="c_pool")
        c_dram = c_words[0].rearrange("p n t -> p (n t)").bitcast(I32)
        nc.sync.dma_start(c_pool[:, :C_AHEAD].bitcast(I32), c_dram[:, :C_AHEAD])

        for unused in (ks_pool[:K_ROWS, :], ks_pool[P // 2 :, :]):
            nc.vector.memset(unused[:, :ODD], 0)
            nc.vector.memset(unused[:, ODD:], 0)
        planes = held.tile([P, 2 * LISTED // 4], I32, name="planes", align_bytes=64)
        nc.gpsimd.memset(planes[:], 0)
        nc.gpsimd.memset(cs_pool[:C_ROWS, :], 0)
        nc.gpsimd.memset(ns_pool[:NS_ROW, :], 0.0)
        identity = held.tile([P, P], F32, name="identity")
        make_identity(nc, identity[:])
        k_plane = planes[:, : LISTED // 4]
        c_plane = planes[:, LISTED // 4 :]

        def listed_offsets(cols):
            return offsets[:, cols.start // PER_COLUMN : cols.stop // PER_COLUMN]

        def gather_scales(name, pool, rows, plane, first, queues):
            listed = held.tile([P, LISTED], U8, name=name, align_bytes=64)
            nc.vector.tensor_copy(listed[:], pool[:].bitcast(U8).indirect(offsets[:]))
            for g, queue in enumerate(queues):
                queue.dma_start(
                    plane[QUADRANT * g + first : QUADRANT * g + first + 4, :],
                    listed[rows + 4 * g : rows + 4 * g + 4, :].bitcast(I32),
                )

        gather_scales("ks_listed", ks_pool, K_ROWS, k_plane, 0, (nc.sync,) * 4)
        nc.sync.dma_start(c_pool[:, C_AHEAD:].bitcast(I32), c_dram[:, C_AHEAD:])
        gather_scales("cs_listed", cs_pool, C_ROWS, c_plane, C_PLANE, (nc.sync,) * 4)

        q_grouped = held.tile([P, NQ, PACK], BF16, name="q_grouped", align_bytes=64)
        nc.scalar.copy(q_grouped[:], q_raw[:].rearrange("p j w -> p w j"))
        ns_listed = held.tile([P, LISTED], F32, name="ns_listed")
        for h in range(2):
            half = slice(h * HALF, (h + 1) * HALF)
            nc.scalar.activation(ns_listed[:, half], ns_pool[:].indirect(listed_offsets(half)), COPY)

        ns_columns = held.tile([P, BLOCKS], F32, name="ns_columns")
        for b in range(BLOCKS):
            turned = psum.tile([P, P], F32, name=f"turned{b}", tag=f"bank{b}")
            nc.tensor.transpose(turned[:], ns_listed[:, b * P : (b + 1) * P], identity[:])
            nc.scalar.copy(ns_columns[:, b : b + 1], turned[:, NS_ROW:P])

        q_codes = in_turn.tile([P, NQ], U32, name="q_codes", align_bytes=64, offset=0)
        q_scales = held.tile([P, NQ], U8, name="q_scales", align_bytes=64)
        nc.vector.quantize_mx(
            out=q_codes[:].bitcast(FP8X4), scales=q_scales[:], in_=q_grouped[:].rearrange("p w j -> p (w j)")
        )

        k_listed = in_turn.tile([P, LISTED], U32, name="k_listed", align_bytes=64, offset=POOL // 2)
        gate = []
        for b in range(BLOCKS):
            if b % 2 == 0:
                half = slice(b * P, b * P + HALF)
                nc.vector.tensor_copy(k_listed[:, half], k_pool[:].indirect(listed_offsets(half)))
            cols = slice(b * P, (b + 1) * P)
            gate.append(psum.tile([P, NQ], F32, name=f"gate{b}", tag=f"bank{b}"))
            nc.tensor.matmul_mx(
                out=gate[b][:],
                lhsT=k_listed[:, cols].bitcast(FP8X4),
                lhsT_scale=k_plane.bitcast(U8)[:, cols],
                rhs=q_codes[:].bitcast(FP8X4),
                rhs_scale=q_scales[:],
                start=True,
                stop=True,
            )
        by_slot = held.tile([P, BLOCKS, NQ], F32, name="by_slot")
        for b in range(BLOCKS):
            nc.scalar.activation(by_slot[:, b, :], gate[b][:], COPY, scale=ns_columns[:, b : b + 1])
        scaled = held.tile([NQ, LISTED], F32, name="scaled")
        for n, cols in enumerate(PIECES):
            back = psum.tile([NQ, cols.stop - cols.start], F32, name=f"back{n}", tag=f"bank{(4, 5, 0)[n]}")
            for b in range(cols.start // P, cols.stop // P):
                nc.tensor.transpose(back[:, b * P - cols.start : (b + 1) * P - cols.start], by_slot[:, b, :], identity[:])
            nc.scalar.copy(scaled[:, cols], back[:])

        c_listed = held.tile([P, LISTED], U32, name="c_listed", align_bytes=64)
        layer = []
        for n, cols in enumerate(PIECES):
            nc.vector.tensor_copy(c_listed[:, cols], c_pool[:].indirect(listed_offsets(cols)))
            layer.append(psum.tile([NQ, cols.stop - cols.start], F32, name=f"layer{n}", tag=f"bank{(6, 7, 1)[n]}"))
            nc.tensor.matmul_mx(
                out=layer[n][:],
                lhsT=q_codes[:].bitcast(FP8X4),
                lhsT_scale=q_scales[:],
                rhs=c_listed[:, cols].bitcast(FP8X4),
                rhs_scale=c_plane.bitcast(U8)[C_PLANE:P, cols],
                start=True,
                stop=True,
            )
        result = held.tile([NQ, LISTED], F32, name="result")
        for n, cols in enumerate(PIECES):
            nc.vector.tensor_tensor(result[:, cols], layer[n][:], scaled[:, cols], MULT)
            queue = nc.scalar if n == 1 else nc.sync
            queue.dma_start(out[0, :, cols], result[:, cols])
